import numpy as np
import ml_dtypes


def mxq(x, axis, fmt="e4m3"):
    dtype, down = {"e4m3": (ml_dtypes.float8_e4m3fn, 7), "e5m2": (ml_dtypes.float8_e5m2, 14)}[fmt]
    v = np.moveaxis(np.asarray(x, np.float32).astype(ml_dtypes.bfloat16).astype(np.float64), axis, -1)
    blocks = v.reshape(v.shape[:-1] + (-1, 32))
    amax = np.abs(blocks).max(-1, keepdims=True)
    byte = np.maximum(np.where(amax > 0, np.frexp(amax)[1] - 1 + 127, 0) - down, 1)
    scale = np.exp2(byte - 127.0)
    codes = (blocks / scale).astype(np.float32).astype(dtype).astype(np.float64)
    return np.moveaxis((codes * scale).reshape(v.shape), -1, axis)


WIDE = False


def mx_kscale(k):
    if not WIDE:
        return np.ones(k)
    levels = np.array([10, -10, 5, -5, 0])
    if k % 512:
        return np.exp2(np.random.permutation(np.resize(levels, k // 32))).repeat(32)
    a = np.empty((k // 512, 16))
    for p in range(k // 512):
        a[p, :8] = np.random.permutation(np.resize(levels, 8))
        for g in range(8):
            far = levels[np.abs(levels - a[p, g]) >= 10]
            a[p, g + 8] = far[np.random.randint(len(far))]
    return np.exp2(a.ravel()).repeat(32)


def f64(x):
    return np.asarray(x).astype(np.float64)


def striped(idx):
    return np.tile(idx.reshape(-1, 16).T, (8, 1)).astype(np.uint16)


def unstriped(offs):
    return offs[:16].T.reshape(-1).astype(np.int64)


E2M1 = np.array([0.0, 0.5, 1.0, 1.5, 2.0, 3.0, 4.0, 6.0, -0.0, -0.5, -1.0, -1.5, -2.0, -3.0, -4.0, -6.0])


def pack_weight(w, fmt):
    k, n = w.shape
    w = f64(np.asarray(w, np.float32).astype(ml_dtypes.bfloat16)).reshape(k // 32, 32, n)
    amax = np.abs(w).max(1)
    if fmt == "e4m3":
        byte = np.frexp(amax)[1] - 1 + 127 - 7
    else:
        mant, ex = np.frexp(amax / 6.0)
        byte = np.where(mant > 0.5, ex, ex - 1) + 127
    byte = np.clip(np.where(amax > 0, byte, 1), 1, 254)
    scaled = (w * np.exp2(127.0 - byte)[:, None, :]).reshape(k, n).astype(np.float32)
    by_word = np.ascontiguousarray(scaled.reshape(k // 512, 128, 4, n).transpose(0, 1, 3, 2))
    if fmt == "e4m3":
        words = by_word.astype(ml_dtypes.float8_e4m3fn).view(np.uint8)
    else:
        c = by_word.astype(ml_dtypes.float4_e2m1fn).view(np.uint8) & 0xF
        words = (c[..., 0::2] | (c[..., 1::2] << 4)).reshape(k // 512, 128, 2 * n)
    return np.ascontiguousarray(words), np.ascontiguousarray(byte.astype(np.uint8).reshape(k // 512, 16, n))


def unpack_weight(words, scales, fmt):
    g, _, n = scales.shape
    words = np.ascontiguousarray(words).reshape(g, 128, n, -1)
    if fmt == "e4m3":
        vals = words.view(ml_dtypes.float8_e4m3fn).astype(np.float64)
    else:
        nib = np.empty((g, 128, n, 4), np.uint8)
        nib[..., 0::2] = words & 0xF
        nib[..., 1::2] = words >> 4
        vals = E2M1[nib]
    vals = vals * np.repeat(np.exp2(scales.astype(np.float64) - 127.0), 8, axis=1)[..., None]
    return vals.transpose(0, 1, 3, 2).reshape(g * 512, n)


def gelu(v):
    return 0.5 * v * (1.0 + np.tanh(np.sqrt(2.0 / np.pi) * (v + 0.044715 * v**3)))


K, H, T, S, T2, P = 1536, 1024, 2048, 512, 1024, 512

def setup_inputs():
    n = np.random.standard_normal
    s = mx_kscale(K)[:, None]
    u = mx_kscale(H)[:, None]
    d = {}
    d["tab_words"], d["tab_scales"] = pack_weight(n((K, T)) * s, "e4m3")
    d["offs"] = striped(np.random.permutation(T)[:S])
    d["wa"] = (1.5 * n((K, H)) / K ** 0.5 / s).astype(np.float32)
    d["w4_words"], d["w4_scales"] = pack_weight(1.5 * n((K, H)) / K ** 0.5 / s, "e2m1")
    d["dough"] = (n((H, S)) * u).astype(np.float32)
    d["wgs"] = np.exp(0.3 * n((128, S))).astype(np.float32)
    d["page0"] = (n((H, T2)) * u).astype(np.float32)
    d["offs2"] = striped(np.random.permutation(T2)[:S])
    d["offs3"] = striped(np.random.permutation(T2)[:P])
    d["w8_words"], d["w8_scales"] = pack_weight(1.2 * n((H, H)) / H ** 0.5 / u * u.T, "e4m3")
    d["floor_v"] = ((0.3 + 0.6 * n(H)) * u[:, 0]).astype(np.float32)
    d["gain"] = (np.sign(n(H)) * np.exp(0.3 * n(H)) / H ** 0.5 / u[:, 0] ** 2).astype(np.float32)
    d["lim"] = (0.5 + n((T2, P))).astype(np.float32)
    return d

def reference(tab_words, tab_scales, offs, wa, w4_words, w4_scales, dough, wgs, page0, offs2, offs3, w8_words, w8_scales, floor_v, gain, lim):
    v = unpack_weight(tab_words, tab_scales, "e4m3")[:, unstriped(offs)]
    w4 = unpack_weight(w4_words, w4_scales, "e2m1")
    w8 = unpack_weight(w8_words, w8_scales, "e4m3")
    fast = mxq(f64(wa), 0, "e4m3").T @ v
    slow = w4.T @ v
    h = np.tanh(np.maximum(fast, slow)) * f64(dough)
    page = f64(page0).copy()
    page[:, unstriped(offs2)] = np.tile(f64(wgs), (H // 128, 1)) * h
    x = page[:, unstriped(offs3)]
    y = w8.T @ mxq(x, 0, "e4m3")
    z = (np.maximum(y, f64(floor_v)[:, None]) + x) * f64(gain)[:, None]
    e = mxq(page, 0, "e4m3").T @ mxq(z, 0, "e4m3")
    return np.abs(np.minimum(e, f64(lim)))

@@ -1,0 +1,350 @@
+from contextlib import ExitStack
+
+import concourse.mybir as mybir
+
+K, H, T, S, T2, NX = 1536, 1024, 2048, 512, 1024, 512
+FLOPS = 2 * (2 * K * H * S + H * H * NX + H * T2 * NX)
+
+F32 = mybir.dt.float32
+BF16 = mybir.dt.bfloat16
+I32 = mybir.dt.int32
+U32 = mybir.dt.uint32
+U16 = mybir.dt.uint16
+U8 = mybir.dt.uint8
+FP8X4 = mybir.dt.float8_e4m3fn_x4
+FP4X4 = mybir.dt.float4_e2m1fn_x4
+ALU = mybir.AluOpType
+ACT = mybir.ActivationFunctionType
+
+P = 128
+KP = K // 512
+HB = H // 512
+CW = 256
+NC = NX // CW
+
+
+def tile_list_pasta_crack_page_kernel(tc, tab_words, tab_scales, offs, wa, w4_words, w4_scales, dough, wgs,
+                                                page0, offs2, offs3, w8_words, w8_scales, floor_v, gain, lim, out):
+    nc = tc.nc
+    with ExitStack() as ctx:
+        keep = ctx.enter_context(tc.tile_pool(name="keep", bufs=1))
+        ring = ctx.enter_context(tc.tile_pool(name="ring", bufs=7))
+        half = ctx.enter_context(tc.tile_pool(name="half", bufs=3))
+        work = ctx.enter_context(tc.tile_pool(name="work", bufs=2))
+        psum = ctx.enter_context(tc.psum_pool(name="psum", bufs=8))
+
+        def kept(shape, dtype, name):
+            return keep.tile(shape, dtype, name=name, align_bytes=64)
+
+        def staged(shape, dtype):
+            return ring.tile(shape, dtype, name="staged", align_bytes=64)
+
+        def rounded(cols):
+            return half.tile([P, cols], BF16, name="rounded", align_bytes=64)
+
+        def bank(cols):
+            return psum.tile([P, cols], F32, name="bank")
+
+        idx = kept([P, S // 16], U16, "idx")
+        idx2 = kept([P, S // 16], U16, "idx2")
+        idx3 = kept([P, NX // 16], U16, "idx3")
+
+        tab_sc = kept([P, T], U8, "tab_sc")
+        w_sc_raw = kept([P, H], U8, "w_sc_raw")
+        nc.vector.memset(tab_sc[:].bitcast(I32), 0)
+        nc.gpsimd.memset(w_sc_raw[:].bitcast(I32), 0)
+        for q in range(4):
+            nc.gpsimd.dma_start(out=w_sc_raw[32 * q + 12 : 32 * q + 20, :].bitcast(I32),
+                                in_=w8_scales[:, 4 * q : 4 * q + 4, :].bitcast(I32))
+
+        def load_scale_rows(dst, src):
+            for q in range(4):
+                nc.sync.dma_start(out=dst[32 * q : 32 * q + 12, :].bitcast(I32), in_=src[:, 4 * q : 4 * q + 4, :].bitcast(I32))
+
+        def shifted(src, rows, name):
+            dst = kept([P, src.shape[1]], U8, name)
+            nc.sync.dma_start(out=dst[0:112, :].bitcast(I32), in_=src[rows : rows + 112, :].bitcast(I32))
+            return dst
+
+        def load_wa(b, a):
+            raw = staged([P, 4, 512], F32)
+            nc.sync.dma_start(out=raw[:], in_=wa[512 * a : 512 * (a + 1), 512 * b : 512 * (b + 1)].rearrange("(p j) c -> p j c", j=4))
+            return raw
+
+        def load_tab(a):
+            words = staged([P, T], I32)
+            nc.sync.dma_start(out=words[:], in_=tab_words[a].rearrange("p t i -> p (t i)").bitcast(I32))
+            return words
+
+        def load_rows4(src, b):
+            rows = staged([P, 4, 512], F32)
+            nc.sync.dma_start(out=rows[:], in_=src[512 * b : 512 * (b + 1), :].rearrange("(p t) c -> p t c", t=4))
+            return rows
+
+        page = {}
+
+        def load_page(b, t):
+            page[b, t] = kept([P, T2], F32, "page%d%d" % (b, t))
+            nc.sync.dma_start(out=page[b, t][:], in_=page0[512 * b : 512 * (b + 1), :].rearrange("(p t) c -> p t c", t=4)[:, t, :])
+
+        wa_raw, tab, dough_t = {}, {}, {}
+        nc.sync.dma_start(idx[:], offs)
+        wa_raw[0, 0] = load_wa(0, 0)
+        load_scale_rows(tab_sc, tab_scales)
+        tab[0] = load_tab(0)
+        wa_raw[0, 1] = load_wa(0, 1)
+        load_scale_rows(w_sc_raw, w4_scales)
+        w4_raw = staged([P, KP, 2 * H], U8)
+        nc.sync.dma_start(out=w4_raw[:].bitcast(I32), in_=w4_words.rearrange("a p c -> p a c").bitcast(I32))
+        tab[1] = load_tab(1)
+        wa_raw[0, 2] = load_wa(0, 2)
+        tab[2] = load_tab(2)
+
+        wa_q, wa_s = {}, {}
+        wa_bf = {}
+
+        def round_wa(b, a):
+            wa_bf[b, a] = rounded(2048)
+            nc.scalar.copy(out=wa_bf[b, a][:].rearrange("p (t m j) -> p m j t", t=4, j=4),
+                           in_=wa_raw[b, a][:].rearrange("p j (m t) -> p m j t", t=4))
+
+        def quantise(src, cols, name):
+            codes = kept([P, cols], U32, name + "_q")
+            scales = kept([P, cols], U8, name + "_s")
+            nc.vector.quantize_mx(out=codes[:].bitcast(FP8X4), scales=scales[:], in_=src[:])
+            return codes, scales
+
+        def quantise_wa(b, a):
+            wa_q[b, a], wa_s[b, a] = quantise(wa_bf[b, a], 512, "wa%d%d" % (b, a))
+
+        v_q, v_s = {}, {}
+
+        def gather_words(a):
+            v_q[a] = kept([P, S], U32, "v_q%d" % a)
+            nc.vector.tensor_copy(v_q[a][:], tab[a][:].bitcast(U32).indirect(idx[:]))
+
+        def gather_scales():
+            v_s[0] = kept([P, S], U8, "v_s0")
+            nc.vector.tensor_copy(v_s[0][:], tab_sc[:].indirect(idx[:]))
+            for a in range(1, KP):
+                v_s[a] = shifted(v_s[0], 4 * a, "v_s%d" % a)
+
+        w_s = {}
+
+        def deal_scales():
+            w_s[0] = kept([P, H], U8, "w_s0")
+            nc.vector.tensor_copy(out=w_s[0][:].rearrange("p (b t m) -> p b t m", b=HB, t=4),
+                                  in_=w_sc_raw[:].rearrange("p (b m t) -> p b t m", b=HB, t=4))
+            for a in range(1, KP):
+                w_s[a] = shifted(w_s[0], 4 * a, "w_s%d" % a)
+
+        w4_q = {}
+
+        def deal_w4(b):
+            w4_q[b] = kept([P, KP, 1024], U8, "w4_q%d" % b)
+            nc.vector.tensor_copy(out=w4_q[b][:].bitcast(U16).rearrange("p a (t m) -> p a t m", t=4),
+                                  in_=w4_raw[:, :, 1024 * b : 1024 * (b + 1)].bitcast(U16).rearrange("p a (m t) -> p a t m", t=4))
+
+        round_wa(0, 0)
+        gather_scales()
+        gather_words(0)
+        round_wa(0, 1)
+        quantise_wa(0, 0)
+        deal_scales()
+        deal_w4(0)
+        gather_words(1)
+        round_wa(0, 2)
+        quantise_wa(0, 1)
+        deal_w4(1)
+        quantise_wa(0, 2)
+        gather_words(2)
+
+        dough_t[0] = load_rows4(dough, 0)
+        wg = kept([P, 4, S], F32, "wg")
+        for u in range(4):
+            nc.sync.dma_start(out=wg[32 * u : 32 * (u + 1)], in_=wgs.rearrange("(v t) s -> v t s", t=4))
+        nc.sync.dma_start(idx2[:], offs2)
+        load_page(0, 0)
+        nc.sync.dma_start(idx3[:], offs3)
+        load_page(0, 1)
+        wa_raw[1, 0] = load_wa(1, 0)
+        load_page(0, 2)
+        wa_raw[1, 1] = load_wa(1, 1)
+        load_page(0, 3)
+        wa_raw[1, 2] = load_wa(1, 2)
+        dough_t[1] = load_rows4(dough, 1)
+        for t in range(4):
+            load_page(1, t)
+        w8_raw = staged([P, HB, H], I32)
+        nc.sync.dma_start(out=w8_raw[:], in_=w8_words.rearrange("a p c i -> p a (c i)").bitcast(I32))
+        floor_t = kept([P, HB, 4], F32, "floor_t")
+        gain_t = kept([P, HB, 4], F32, "gain_t")
+        nc.sync.dma_start(out=floor_t[:], in_=floor_v.rearrange("(b p t) -> p b t", b=HB, t=4))
+        nc.sync.dma_start(out=gain_t[:], in_=gain.rearrange("(b p t) -> p b t", b=HB, t=4))
+        lim_t = {}
+        for mh in range(2):
+            lim_t[mh] = staged([P, 4, NX], F32)
+            nc.sync.dma_start(out=lim_t[mh][:], in_=lim[512 * mh : 512 * (mh + 1), :].rearrange("(g p) j -> p g j", p=P))
+
+        tiles = [(b, t) for b in range(HB) for t in range(4)]
+        top, crack = {}, {}
+
+        def readings(i):
+            b, t = tiles[i]
+            slow = bank(S)
+            for a in range(KP):
+                nc.tensor.matmul_mx(out=slow[:], lhsT=w4_q[b][:, a, 256 * t : 256 * (t + 1)].bitcast(FP4X4),
+                                    lhsT_scale=w_s[a][:, 512 * b + P * t : 512 * b + P * (t + 1)],
+                                    rhs=v_q[a][:].bitcast(FP8X4), rhs_scale=v_s[a][:], start=(a == 0), stop=(a == KP - 1))
+            fast = bank(S)
+            for a in range(KP):
+                nc.tensor.matmul_mx(out=fast[:], lhsT=wa_q[b, a][:, P * t : P * (t + 1)].bitcast(FP8X4),
+                                    lhsT_scale=wa_s[b, a][:, P * t : P * (t + 1)],
+                                    rhs=v_q[a][:].bitcast(FP8X4), rhs_scale=v_s[a][:], start=(a == 0), stop=(a == KP - 1))
+            slow_sb = work.tile([P, S], F32, name="slow_sb")
+            nc.scalar.copy(out=slow_sb[:], in_=slow[:])
+            top[i] = work.tile([P, S], F32, name="top")
+            nc.vector.tensor_tensor(top[i][:], fast[:], slow_sb[:], ALU.max)
+            nc.scalar.activation(top[i][:], top[i][:], ACT.Tanh)
+
+        def times_dough(i):
+            b, t = tiles[i]
+            crack[i] = work.tile([P, S], F32, name="crack")
+            nc.vector.tensor_tensor(crack[i][:], top[i][:], dough_t[b][:, t, :], ALU.mult)
+
+        planes = {}
+
+        def put(i):
+            b, t = tiles[i]
+            nc.vector.tensor_tensor(page[b, t][:].indirect(idx2[:]), crack[i][:], wg[:, t, :], ALU.mult)
+
+        def round_page_row(i):
+            b, t = tiles[i]
+            if t == 0:
+                planes[b] = work.tile([P, 4, T2], BF16, name="planes", bufs=1)
+            nc.scalar.copy(out=planes[b][:, t, :], in_=page[b, t][:])
+
+        x = {(b, c): kept([P, 4, CW], F32, "x%d%d" % (b, c)) for b in range(HB) for c in range(NC)}
+
+        def fetch(i, c):
+            b, t = tiles[i]
+            nc.vector.tensor_copy(x[b, c][:, t, :], page[b, t][:].indirect(idx3[:, c * CW // 16 : (c + 1) * CW // 16]))
+
+        x_bf, x_q, x_s = {}, {}, {}
+
+        def round_x(b, c):
+            x_bf[b, c] = rounded(4 * CW)
+            nc.scalar.copy(out=x_bf[b, c][:].rearrange("p (c i t) -> p c t i", i=4, t=4),
+                           in_=x[b, c][:].rearrange("p t (c i) -> p c t i", i=4))
+
+        def quantise_x(b, c):
+            x_q[b, c], x_s[b, c] = quantise(x_bf[b, c], CW, "x%d%d" % (b, c))
+
+        page_bf, page_q, page_s = {}, {}, {}
+
+        def weave_page(b, mh):
+            page_bf[b, mh] = rounded(2048)
+            nc.scalar.copy(out=page_bf[b, mh][:].rearrange("p (c i t) -> p c t i", i=4, t=4),
+                           in_=planes[b][:, :, 512 * mh : 512 * (mh + 1)].rearrange("p t (c i) -> p c t i", i=4))
+
+        def quantise_page(b, mh):
+            page_q[b, mh], page_s[b, mh] = quantise(page_bf[b, mh], 512, "page%d%d" % (b, mh))
+
+        w8_q = kept([P, HB, H], U32, "w8_q")
+
+        def deal_w8():
+            nc.vector.tensor_copy(out=w8_q[:].rearrange("p a (b t m) -> p (a b) m t", b=HB, t=4),
+                                  in_=w8_raw[:].bitcast(U32).rearrange("p a (b m t) -> p (a b) m t", b=HB, t=4))
+
+        readings(0)
+        readings(1)
+        times_dough(0)
+        for i in range(8):
+            put(i)
+            if i < 3:
+                round_wa(1, i)
+            if i + 1 < 8:
+                times_dough(i + 1)
+            if 1 <= i <= 2:
+                quantise_wa(1, i - 1)
+            if i == 2:
+                quantise_wa(1, 2)
+            if i + 2 < 8:
+                readings(i + 2)
+            fetch(i, 0)
+            if i == 7:
+                round_x(1, 0)
+            fetch(i, 1)
+            if i == 7:
+                round_x(1, 1)
+            round_page_row(i)
+            if i == 3:
+                round_x(0, 0)
+                round_x(0, 1)
+            if i == 4:
+                quantise_x(0, 0)
+                quantise_x(0, 1)
+                weave_page(0, 0)
+            if i == 5:
+                quantise_page(0, 0)
+                weave_page(0, 1)
+                deal_w8()
+            if i == 6:
+                quantise_page(0, 1)
+
+        z_bf, z_q, z_s = {}, {}, {}
+
+        def lift(b, c):
+            for t in range(4):
+                y = bank(CW)
+                col = 512 * b + P * t
+                for a in range(HB):
+                    nc.tensor.matmul_mx(out=y[:], lhsT=w8_q[:, a, col : col + P].bitcast(FP8X4),
+                                        lhsT_scale=w_s[a][12:P, col : col + P],
+                                        rhs=x_q[a, c][:].bitcast(FP8X4), rhs_scale=x_s[a, c][:], start=(a == 0), stop=(a == HB - 1))
+                nc.vector.scalar_tensor_tensor(x[b, c][:, t, :], y[:], floor_t[:, b, t : t + 1], x[b, c][:, t, :], ALU.max, ALU.add)
+
+        def round_z(b, c):
+            z_bf[b, c] = rounded(4 * CW)
+            nc.vector.tensor_tensor(z_bf[b, c][:].rearrange("p (c i t) -> p c t i", i=4, t=4),
+                                    x[b, c][:].rearrange("p t (c i) -> p c t i", i=4),
+                                    gain_t[:, b, :].unsqueeze(1).unsqueeze(3).to_broadcast([P, CW // 4, 4, 4]), ALU.mult)
+
+        def quantise_z(b, c):
+            z_q[b, c], z_s[b, c] = quantise(z_bf[b, c], CW, "z%d%d" % (b, c))
+
+        def score(c, mh):
+            cols = slice(c * CW, (c + 1) * CW)
+            for g in range(4):
+                e = bank(CW)
+                for b in range(HB):
+                    nc.tensor.matmul_mx(out=e[:], lhsT=page_q[b, mh][:, P * g : P * (g + 1)].bitcast(FP8X4),
+                                        lhsT_scale=page_s[b, mh][:, P * g : P * (g + 1)],
+                                        rhs=z_q[b, c][:].bitcast(FP8X4), rhs_scale=z_s[b, c][:], start=(b == 0), stop=(b == HB - 1))
+                nc.vector.tensor_tensor(lim_t[mh][:, g, cols], e[:], lim_t[mh][:, g, cols], ALU.min)
+                nc.scalar.activation(lim_t[mh][:, g, cols], lim_t[mh][:, g, cols], ACT.Abs)
+                row = 512 * mh + P * g
+                nc.sync.dma_start(out=out[row : row + P, cols], in_=lim_t[mh][:, g, cols])
+
+        quantise_x(1, 0)
+        weave_page(1, 0)
+        quantise_x(1, 1)
+        weave_page(1, 1)
+        lift(0, 0)
+        lift(1, 0)
+        round_z(0, 0)
+        round_z(1, 0)
+        quantise_z(0, 0)
+        quantise_page(1, 0)
+        quantise_z(1, 0)
+        lift(0, 1)
+        lift(1, 1)
+        quantise_page(1, 1)
+        round_z(0, 1)
+        score(0, 0)
+        round_z(1, 1)
+        quantise_z(0, 1)
+        score(0, 1)
+        quantise_z(1, 1)
+        score(1, 0)
+        score(1, 1)

@@ -49,21 +49,23 @@ def tile_list_pasta_crack_page_kernel(tc, tab_words, tab_scales, offs, wa, w4_wo
         idx2 = kept([P, S // 16], U16, "idx2")
         idx3 = kept([P, NX // 16], U16, "idx3")
 
-        tab_sc = kept([P, T], U8, "tab_sc")
-        w_sc_raw = kept([P, H], U8, "w_sc_raw")
-        nc.vector.memset(tab_sc[:].bitcast(I32), 0)
-        nc.gpsimd.memset(w_sc_raw[:].bitcast(I32), 0)
-        for q in range(4):
-            nc.gpsimd.dma_start(out=w_sc_raw[32 * q + 12 : 32 * q + 20, :].bitcast(I32),
-                                in_=w8_scales[:, 4 * q : 4 * q + 4, :].bitcast(I32))
+        tab_sc = keep.tile([P, T], U8, name="tab_sc", tag="scale_rows", align_bytes=64)
+        w4_sc_raw = kept([P, KP, H], U8, "w4_sc_raw")
+        nc.gpsimd.memset(tab_sc[:].bitcast(I32), 0)
+        nc.vector.memset(w4_sc_raw[:].rearrange("p a c -> p (a c)").bitcast(I32), 0)
 
         def load_scale_rows(dst, src):
             for q in range(4):
-                nc.sync.dma_start(out=dst[32 * q : 32 * q + 12, :].bitcast(I32), in_=src[:, 4 * q : 4 * q + 4, :].bitcast(I32))
+                nc.gpsimd.dma_start(out=dst[32 * q : 32 * q + 4 * src.shape[0], :].bitcast(I32), in_=src[:, 4 * q : 4 * q + 4, :].bitcast(I32))
+
+        load_scale_rows(tab_sc, tab_scales)
+        for q in range(4):
+            nc.gpsimd.dma_start(out=w4_sc_raw[32 * q : 32 * q + 4].bitcast(I32),
+                                in_=w4_scales[:, 4 * q : 4 * q + 4, :].rearrange("a r c -> r a c").bitcast(I32))
 
         def shifted(src, rows, name):
             dst = kept([P, src.shape[1]], U8, name)
-            nc.sync.dma_start(out=dst[0:112, :].bitcast(I32), in_=src[rows : rows + 112, :].bitcast(I32))
+            nc.gpsimd.dma_start(out=dst[0:112, :].bitcast(I32), in_=src[rows : rows + 112, :].bitcast(I32))
             return dst
 
         def load_wa(b, a):
@@ -81,6 +83,13 @@ def tile_list_pasta_crack_page_kernel(tc, tab_words, tab_scales, offs, wa, w4_wo
             nc.sync.dma_start(out=rows[:], in_=src[512 * b : 512 * (b + 1), :].rearrange("(p t) c -> p t c", t=4))
             return rows
 
+        w4_raw = {}
+
+        def load_w4(b):
+            w4_raw[b] = staged([P, KP, H], U8)
+            nc.sync.dma_start(out=w4_raw[b][:].bitcast(I32),
+                              in_=w4_words[:, :, H * b : H * (b + 1)].rearrange("a p c -> p a c").bitcast(I32))
+
         page = {}
 
         def load_page(b, t):
@@ -89,13 +98,10 @@ def tile_list_pasta_crack_page_kernel(tc, tab_words, tab_scales, offs, wa, w4_wo
 
         wa_raw, tab, dough_t = {}, {}, {}
         nc.sync.dma_start(idx[:], offs)
+        load_w4(0)
         wa_raw[0, 0] = load_wa(0, 0)
-        load_scale_rows(tab_sc, tab_scales)
         tab[0] = load_tab(0)
         wa_raw[0, 1] = load_wa(0, 1)
-        load_scale_rows(w_sc_raw, w4_scales)
-        w4_raw = staged([P, KP, 2 * H], U8)
-        nc.sync.dma_start(out=w4_raw[:].bitcast(I32), in_=w4_words.rearrange("a p c -> p a c").bitcast(I32))
         tab[1] = load_tab(1)
         wa_raw[0, 2] = load_wa(0, 2)
         tab[2] = load_tab(2)
@@ -129,43 +135,52 @@ def tile_list_pasta_crack_page_kernel(tc, tab_words, tab_scales, offs, wa, w4_wo
             for a in range(1, KP):
                 v_s[a] = shifted(v_s[0], 4 * a, "v_s%d" % a)
 
-        w_s = {}
+        w4_s = {}
 
-        def deal_scales():
-            w_s[0] = kept([P, H], U8, "w_s0")
-            nc.vector.tensor_copy(out=w_s[0][:].rearrange("p (b t m) -> p b t m", b=HB, t=4),
-                                  in_=w_sc_raw[:].rearrange("p (b m t) -> p b t m", b=HB, t=4))
-            for a in range(1, KP):
-                w_s[a] = shifted(w_s[0], 4 * a, "w_s%d" % a)
+        def deal_w4_scales(b):
+            w4_s[b] = kept([P, KP, 512], U8, "w4_s%d" % b)
+            nc.vector.tensor_copy(out=w4_s[b][:].rearrange("p a (t m) -> p a t m", t=4),
+                                  in_=w4_sc_raw[:, :, 512 * b : 512 * (b + 1)].rearrange("p a (m t) -> p a t m", t=4))
 
         w4_q = {}
 
         def deal_w4(b):
             w4_q[b] = kept([P, KP, 1024], U8, "w4_q%d" % b)
             nc.vector.tensor_copy(out=w4_q[b][:].bitcast(U16).rearrange("p a (t m) -> p a t m", t=4),
-                                  in_=w4_raw[:, :, 1024 * b : 1024 * (b + 1)].bitcast(U16).rearrange("p a (m t) -> p a t m", t=4))
+                                  in_=w4_raw[b][:].bitcast(U16).rearrange("p a (m t) -> p a t m", t=4))
 
         round_wa(0, 0)
+        deal_w4(0)
         gather_scales()
+        w8_sc_raw = keep.tile([P, H], U8, name="w8_sc_raw", tag="scale_rows", align_bytes=64)
+        nc.gpsimd.memset(w8_sc_raw[:].bitcast(I32), 0)
+        load_scale_rows(w8_sc_raw, w8_scales)
         gather_words(0)
         round_wa(0, 1)
         quantise_wa(0, 0)
-        deal_scales()
-        deal_w4(0)
+        deal_w4_scales(0)
         gather_words(1)
         round_wa(0, 2)
         quantise_wa(0, 1)
-        deal_w4(1)
         quantise_wa(0, 2)
         gather_words(2)
 
-        dough_t[0] = load_rows4(dough, 0)
-        wg = kept([P, 4, S], F32, "wg")
+        load_w4(1)
+        dough_rows = dough.rearrange("(b p t) s -> b p t s", b=HB, t=4)
+        dough_first = kept([P, S], F32, "dough_first")
+        nc.sync.dma_start(out=dough_first[:], in_=dough_rows[0, :, 0, :])
+        wgs_rows = wgs.rearrange("(v t) s -> v t s", t=4)
+        wg_first = kept([P, S], F32, "wg_first")
         for u in range(4):
-            nc.sync.dma_start(out=wg[32 * u : 32 * (u + 1)], in_=wgs.rearrange("(v t) s -> v t s", t=4))
+            nc.sync.dma_start(out=wg_first[32 * u : 32 * (u + 1)], in_=wgs_rows[:, 0, :])
         nc.sync.dma_start(idx2[:], offs2)
         load_page(0, 0)
         nc.sync.dma_start(idx3[:], offs3)
+        dough_rest = staged([P, 3, S], F32)
+        nc.sync.dma_start(out=dough_rest[:], in_=dough_rows[0, :, 1:4, :])
+        wg_rest = keep.tile([P, 3, S], F32, name="wg_rest", tag="late", align_bytes=64)
+        for u in range(4):
+            nc.sync.dma_start(out=wg_rest[32 * u : 32 * (u + 1)], in_=wgs_rows[:, 1:4, :])
         load_page(0, 1)
         wa_raw[1, 0] = load_wa(1, 0)
         load_page(0, 2)
@@ -192,31 +207,32 @@ def tile_list_pasta_crack_page_kernel(tc, tab_words, tab_scales, offs, wa, w4_wo
         def readings(i):
             b, t = tiles[i]
             slow = bank(S)
-            for a in range(KP):
-                nc.tensor.matmul_mx(out=slow[:], lhsT=w4_q[b][:, a, 256 * t : 256 * (t + 1)].bitcast(FP4X4),
-                                    lhsT_scale=w_s[a][:, 512 * b + P * t : 512 * b + P * (t + 1)],
-                                    rhs=v_q[a][:].bitcast(FP8X4), rhs_scale=v_s[a][:], start=(a == 0), stop=(a == KP - 1))
             fast = bank(S)
             for a in range(KP):
+                nc.tensor.matmul_mx(out=slow[:], lhsT=w4_q[b][:, a, 256 * t : 256 * (t + 1)].bitcast(FP4X4),
+                                    lhsT_scale=w4_s[b][:, a, P * t : P * (t + 1)],
+                                    rhs=v_q[a][:].bitcast(FP8X4), rhs_scale=v_s[a][:], start=(a == 0), stop=(a == KP - 1))
                 nc.tensor.matmul_mx(out=fast[:], lhsT=wa_q[b, a][:, P * t : P * (t + 1)].bitcast(FP8X4),
                                     lhsT_scale=wa_s[b, a][:, P * t : P * (t + 1)],
                                     rhs=v_q[a][:].bitcast(FP8X4), rhs_scale=v_s[a][:], start=(a == 0), stop=(a == KP - 1))
             slow_sb = work.tile([P, S], F32, name="slow_sb")
             nc.scalar.copy(out=slow_sb[:], in_=slow[:])
-            top[i] = work.tile([P, S], F32, name="top")
+            top[i] = work.tile([P, S], F32, name="top", bufs=3)
             nc.vector.tensor_tensor(top[i][:], fast[:], slow_sb[:], ALU.max)
             nc.scalar.activation(top[i][:], top[i][:], ACT.Tanh)
 
         def times_dough(i):
             b, t = tiles[i]
             crack[i] = work.tile([P, S], F32, name="crack")
-            nc.vector.tensor_tensor(crack[i][:], top[i][:], dough_t[b][:, t, :], ALU.mult)
+            rows = dough_t[1][:, t, :] if b == 1 else dough_rest[:, t - 1, :] if t > 0 else dough_first[:]
+            engine = nc.vector if i == 0 else nc.gpsimd
+            engine.tensor_tensor(crack[i][:], top[i][:], rows, ALU.mult)
 
         planes = {}
 
         def put(i):
             b, t = tiles[i]
-            nc.vector.tensor_tensor(page[b, t][:].indirect(idx2[:]), crack[i][:], wg[:, t, :], ALU.mult)
+            nc.vector.tensor_tensor(page[b, t][:].indirect(idx2[:]), crack[i][:], wg_rest[:, t - 1, :] if t > 0 else wg_first[:], ALU.mult)
 
         def round_page_row(i):
             b, t = tiles[i]
@@ -224,38 +240,52 @@ def tile_list_pasta_crack_page_kernel(tc, tab_words, tab_scales, offs, wa, w4_wo
                 planes[b] = work.tile([P, 4, T2], BF16, name="planes", bufs=1)
             nc.scalar.copy(out=planes[b][:, t, :], in_=page[b, t][:])
 
-        x = {(b, c): kept([P, 4, CW], F32, "x%d%d" % (b, c)) for b in range(HB) for c in range(NC)}
+        x_whole = kept([P, 4, NX], F32, "x_whole")
+        x = {(0, c): x_whole[:, :, c * CW : (c + 1) * CW] for c in range(NC)}
+        for c in range(NC):
+            x[1, c] = kept([P, 4, CW], F32, "x1%d" % c)[:]
 
-        def fetch(i, c):
-            b, t = tiles[i]
-            nc.vector.tensor_copy(x[b, c][:, t, :], page[b, t][:].indirect(idx3[:, c * CW // 16 : (c + 1) * CW // 16]))
+        def fetch_whole(t):
+            nc.vector.tensor_copy(x_whole[:, t, :], page[0, t][:].indirect(idx3[:]))
+
+        def fetch(t, c):
+            nc.vector.tensor_copy(x[1, c][:, t, :], page[1, t][:].indirect(idx3[:, c * CW // 16 : (c + 1) * CW // 16]))
 
         x_bf, x_q, x_s = {}, {}, {}
 
         def round_x(b, c):
             x_bf[b, c] = rounded(4 * CW)
             nc.scalar.copy(out=x_bf[b, c][:].rearrange("p (c i t) -> p c t i", i=4, t=4),
-                           in_=x[b, c][:].rearrange("p t (c i) -> p c t i", i=4))
+                           in_=x[b, c].rearrange("p t (c i) -> p c t i", i=4))
 
         def quantise_x(b, c):
             x_q[b, c], x_s[b, c] = quantise(x_bf[b, c], CW, "x%d%d" % (b, c))
 
         page_bf, page_q, page_s = {}, {}, {}
 
-        def weave_page(b, mh):
-            page_bf[b, mh] = rounded(2048)
-            nc.scalar.copy(out=page_bf[b, mh][:].rearrange("p (c i t) -> p c t i", i=4, t=4),
-                           in_=planes[b][:, :, 512 * mh : 512 * (mh + 1)].rearrange("p t (c i) -> p c t i", i=4))
+        def weave_page(b, mh, rows):
+            page_bf[b, mh] = rounded(2048) if b == 0 else kept([P, 2048], BF16, "page_bf%d" % mh)
+            nc.scalar.copy(out=page_bf[b, mh][:].rearrange("p (c i t) -> p c t i", i=4, t=4)[:, :, 0:rows, :],
+                           in_=planes[b][:, 0:rows, 512 * mh : 512 * (mh + 1)].rearrange("p t (c i) -> p c t i", i=4))
+
+        def weave_last_row(mh):
+            nc.scalar.copy(out=page_bf[1, mh][:].rearrange("p (m t) -> p m t", t=4)[:, :, 3],
+                           in_=page[1, 3][:, 512 * mh : 512 * (mh + 1)])
 
         def quantise_page(b, mh):
             page_q[b, mh], page_s[b, mh] = quantise(page_bf[b, mh], 512, "page%d%d" % (b, mh))
 
-        w8_q = kept([P, HB, H], U32, "w8_q")
+        w8_s = kept([P, H], U8, "w8_s")
 
-        def deal_w8():
-            nc.vector.tensor_copy(out=w8_q[:].rearrange("p a (b t m) -> p (a b) m t", b=HB, t=4),
-                                  in_=w8_raw[:].bitcast(U32).rearrange("p a (b m t) -> p (a b) m t", b=HB, t=4))
+        def deal_w8(b):
+            cols = slice(512 * b, 512 * (b + 1))
+            nc.vector.tensor_copy(out=w8_q[:, :, cols].rearrange("p a (t m) -> p a m t", t=4),
+                                  in_=w8_raw[:, :, cols].bitcast(U32).rearrange("p a (m t) -> p a m t", t=4))
 
+        deal_w4(1)
+        deal_w4_scales(1)
+        nc.vector.tensor_copy(out=w8_s[:].rearrange("p (b t m) -> p b t m", b=HB, t=4),
+                              in_=w8_sc_raw[:].rearrange("p (b m t) -> p b t m", b=HB, t=4))
         readings(0)
         readings(1)
         times_dough(0)
@@ -265,32 +295,38 @@ def tile_list_pasta_crack_page_kernel(tc, tab_words, tab_scales, offs, wa, w4_wo
                 round_wa(1, i)
             if i + 1 < 8:
                 times_dough(i + 1)
-            if 1 <= i <= 2:
-                quantise_wa(1, i - 1)
-            if i == 2:
-                quantise_wa(1, 2)
             if i + 2 < 8:
+                if i == 2:
+                    quantise_wa(1, 2)
                 readings(i + 2)
-            fetch(i, 0)
-            if i == 7:
-                round_x(1, 0)
-            fetch(i, 1)
-            if i == 7:
-                round_x(1, 1)
-            round_page_row(i)
+            if i < 4:
+                fetch_whole(i)
+            else:
+                fetch(i - 4, 0)
+                if i == 7:
+                    round_x(1, 0)
+                fetch(i - 4, 1)
+                if i == 7:
+                    round_x(1, 1)
+            if i < 2:
+                quantise_wa(1, i)
+            if i < 7:
+                round_page_row(i)
             if i == 3:
                 round_x(0, 0)
                 round_x(0, 1)
             if i == 4:
                 quantise_x(0, 0)
                 quantise_x(0, 1)
-                weave_page(0, 0)
+                weave_page(0, 0, 4)
             if i == 5:
                 quantise_page(0, 0)
-                weave_page(0, 1)
-                deal_w8()
+                weave_page(0, 1, 4)
             if i == 6:
                 quantise_page(0, 1)
+                weave_page(1, 0, 3)
+                weave_page(1, 1, 3)
+        w8_q = keep.tile([P, HB, H], U32, name="w8_q", tag="late", align_bytes=64)
 
         z_bf, z_q, z_s = {}, {}, {}
 
@@ -300,51 +336,63 @@ def tile_list_pasta_crack_page_kernel(tc, tab_words, tab_scales, offs, wa, w4_wo
                 col = 512 * b + P * t
                 for a in range(HB):
                     nc.tensor.matmul_mx(out=y[:], lhsT=w8_q[:, a, col : col + P].bitcast(FP8X4),
-                                        lhsT_scale=w_s[a][12:P, col : col + P],
+                                        lhsT_scale=w8_s[4 * a : P, col : col + P],
                                         rhs=x_q[a, c][:].bitcast(FP8X4), rhs_scale=x_s[a, c][:], start=(a == 0), stop=(a == HB - 1))
                 nc.vector.scalar_tensor_tensor(x[b, c][:, t, :], y[:], floor_t[:, b, t : t + 1], x[b, c][:, t, :], ALU.max, ALU.add)
 
         def round_z(b, c):
             z_bf[b, c] = rounded(4 * CW)
             nc.vector.tensor_tensor(z_bf[b, c][:].rearrange("p (c i t) -> p c t i", i=4, t=4),
-                                    x[b, c][:].rearrange("p t (c i) -> p c t i", i=4),
+                                    x[b, c].rearrange("p t (c i) -> p c t i", i=4),
                                     gain_t[:, b, :].unsqueeze(1).unsqueeze(3).to_broadcast([P, CW // 4, 4, 4]), ALU.mult)
+
+        def round_z_on_scalar(b, c):
+            z_rows = work.tile([P, 4, CW], BF16, name="z_rows")
+            for t in range(4):
+                nc.scalar.activation(z_rows[:, t, :], x[b, c][:, t, :], ACT.Copy, scale=gain_t[:, b, t : t + 1])
+            z_bf[b, c] = rounded(4 * CW)
+            nc.scalar.copy(out=z_bf[b, c][:].rearrange("p (c i t) -> p c t i", i=4, t=4),
+                           in_=z_rows[:].rearrange("p t (c i) -> p c t i", i=4))
 
         def quantise_z(b, c):
             z_q[b, c], z_s[b, c] = quantise(z_bf[b, c], CW, "z%d%d" % (b, c))
 
         def score(c, mh):
             cols = slice(c * CW, (c + 1) * CW)
-            for g in range(4):
-                e = bank(CW)
-                for b in range(HB):
-                    nc.tensor.matmul_mx(out=e[:], lhsT=page_q[b, mh][:, P * g : P * (g + 1)].bitcast(FP8X4),
-                                        lhsT_scale=page_s[b, mh][:, P * g : P * (g + 1)],
-                                        rhs=z_q[b, c][:].bitcast(FP8X4), rhs_scale=z_s[b, c][:], start=(b == 0), stop=(b == HB - 1))
-                nc.vector.tensor_tensor(lim_t[mh][:, g, cols], e[:], lim_t[mh][:, g, cols], ALU.min)
-                nc.scalar.activation(lim_t[mh][:, g, cols], lim_t[mh][:, g, cols], ACT.Abs)
-                row = 512 * mh + P * g
-                nc.sync.dma_start(out=out[row : row + P, cols], in_=lim_t[mh][:, g, cols])
+            for g0 in (0, 2):
+                e = psum.tile([P, 2, CW], F32, name="bank")
+                for g in (g0, g0 + 1):
+                    for b in range(HB):
+                        nc.tensor.matmul_mx(out=e[:, g - g0, :], lhsT=page_q[b, mh][:, P * g : P * (g + 1)].bitcast(FP8X4),
+                                            lhsT_scale=page_s[b, mh][:, P * g : P * (g + 1)],
+                                            rhs=z_q[b, c][:].bitcast(FP8X4), rhs_scale=z_s[b, c][:], start=(b == 0), stop=(b == HB - 1))
+                result = lim_t[mh][:, g0 : g0 + 2, cols]
+                nc.vector.tensor_tensor(result, e[:], result, ALU.min)
+                nc.scalar.activation(result, result, ACT.Abs)
+                row = 512 * mh + P * g0
+                nc.sync.dma_start(out=out[row : row + 2 * P, cols].rearrange("(g p) j -> p g j", p=P), in_=result)
 
+        deal_w8(0)
         quantise_x(1, 0)
-        weave_page(1, 0)
+        weave_last_row(0)
+        deal_w8(1)
         quantise_x(1, 1)
-        weave_page(1, 1)
         lift(0, 0)
+        round_z_on_scalar(0, 0)
+        weave_last_row(1)
         lift(1, 0)
-        round_z(0, 0)
         round_z(1, 0)
-        quantise_z(0, 0)
-        quantise_page(1, 0)
-        quantise_z(1, 0)
         lift(0, 1)
+        round_z_on_scalar(0, 1)
+        quantise_z(0, 0)
+        quantise_z(1, 0)
+        quantise_page(1, 0)
         lift(1, 1)
-        quantise_page(1, 1)
-        round_z(0, 1)
-        score(0, 0)
         round_z(1, 1)
+        score(0, 0)
+        quantise_page(1, 1)
         quantise_z(0, 1)
-        score(0, 1)
         quantise_z(1, 1)
+        score(0, 1)
         score(1, 0)
         score(1, 1)

@@ -28,7 +28,7 @@ def tile_list_pasta_crack_page_kernel(tc, tab_words, tab_scales, offs, wa, w4_wo
     nc = tc.nc
     with ExitStack() as ctx:
         keep = ctx.enter_context(tc.tile_pool(name="keep", bufs=1))
-        ring = ctx.enter_context(tc.tile_pool(name="ring", bufs=7))
+        ring = ctx.enter_context(tc.tile_pool(name="ring", bufs=3))
         half = ctx.enter_context(tc.tile_pool(name="half", bufs=3))
         work = ctx.enter_context(tc.tile_pool(name="work", bufs=2))
         psum = ctx.enter_context(tc.psum_pool(name="psum", bufs=8))
@@ -36,8 +36,8 @@ def tile_list_pasta_crack_page_kernel(tc, tab_words, tab_scales, offs, wa, w4_wo
         def kept(shape, dtype, name):
             return keep.tile(shape, dtype, name=name, align_bytes=64)
 
-        def staged(shape, dtype):
-            return ring.tile(shape, dtype, name="staged", align_bytes=64)
+        def staged(shape, dtype, tag, bufs=3):
+            return ring.tile(shape, dtype, name=tag, tag=tag, bufs=bufs, align_bytes=64)
 
         def rounded(cols):
             return half.tile([P, cols], BF16, name="rounded", align_bytes=64)
@@ -49,68 +49,57 @@ def tile_list_pasta_crack_page_kernel(tc, tab_words, tab_scales, offs, wa, w4_wo
         idx2 = kept([P, S // 16], U16, "idx2")
         idx3 = kept([P, NX // 16], U16, "idx3")
 
-        tab_sc = keep.tile([P, T], U8, name="tab_sc", tag="scale_rows", align_bytes=64)
-        w4_sc_raw = kept([P, KP, H], U8, "w4_sc_raw")
-        nc.gpsimd.memset(tab_sc[:].bitcast(I32), 0)
-        nc.vector.memset(w4_sc_raw[:].rearrange("p a c -> p (a c)").bitcast(I32), 0)
+        tab_sc = keep.tile([P, KP, T], U8, name="tab_sc", tag="scale_rows", align_bytes=64)
+        w4_sc_raw = staged([P, KP, H], U8, "w4_scale_slot", 1)
+        nc.gpsimd.memset(tab_sc[:, 0, :].bitcast(I32), 0)
+        nc.vector.memset(tab_sc[:, 1:KP, :].rearrange("p a c -> p (a c)").bitcast(I32), 0)
+        nc.gpsimd.memset(w4_sc_raw[:].rearrange("p a c -> p (a c)").bitcast(I32), 0)
 
-        def load_scale_rows(dst, src):
-            for q in range(4):
-                nc.gpsimd.dma_start(out=dst[32 * q : 32 * q + 4 * src.shape[0], :].bitcast(I32), in_=src[:, 4 * q : 4 * q + 4, :].bitcast(I32))
-
-        load_scale_rows(tab_sc, tab_scales)
-        for q in range(4):
-            nc.gpsimd.dma_start(out=w4_sc_raw[32 * q : 32 * q + 4].bitcast(I32),
-                                in_=w4_scales[:, 4 * q : 4 * q + 4, :].rearrange("a r c -> r a c").bitcast(I32))
-
-        def shifted(src, rows, name):
-            dst = kept([P, src.shape[1]], U8, name)
-            nc.gpsimd.dma_start(out=dst[0:112, :].bitcast(I32), in_=src[rows : rows + 112, :].bitcast(I32))
-            return dst
+        def load_scale_rows(dst, src, quadrants):
+            for q in quadrants:
+                nc.sync.dma_start(out=dst[32 * q : 32 * q + 4].bitcast(I32),
+                                in_=src[:, 4 * q : 4 * q + 4, :].rearrange("a r c -> r a c").bitcast(I32))
 
         def load_wa(b, a):
-            raw = staged([P, 4, 512], F32)
+            raw = staged([P, 4, 512], F32, "wa_slot")
             nc.sync.dma_start(out=raw[:], in_=wa[512 * a : 512 * (a + 1), 512 * b : 512 * (b + 1)].rearrange("(p j) c -> p j c", j=4))
             return raw
 
         def load_tab(a):
-            words = staged([P, T], I32)
+            words = staged([P, T], I32, "tab_slot") if a < KP - 1 else staged([P, T], I32, "last_tab_slot", 1)
             nc.sync.dma_start(out=words[:], in_=tab_words[a].rearrange("p t i -> p (t i)").bitcast(I32))
             return words
 
-        def load_rows4(src, b):
-            rows = staged([P, 4, 512], F32)
-            nc.sync.dma_start(out=rows[:], in_=src[512 * b : 512 * (b + 1), :].rearrange("(p t) c -> p t c", t=4))
-            return rows
-
-        w4_raw = {}
-
-        def load_w4(b):
-            w4_raw[b] = staged([P, KP, H], U8)
-            nc.sync.dma_start(out=w4_raw[b][:].bitcast(I32),
-                              in_=w4_words[:, :, H * b : H * (b + 1)].rearrange("a p c -> p a c").bitcast(I32))
-
         page = {}
 
-        def load_page(b, t):
-            page[b, t] = kept([P, T2], F32, "page%d%d" % (b, t))
-            nc.sync.dma_start(out=page[b, t][:], in_=page0[512 * b : 512 * (b + 1), :].rearrange("(p t) c -> p t c", t=4)[:, t, :])
+        def load_page(b, t, tile):
+            page[b, t] = tile
+            nc.sync.dma_start(out=tile[:], in_=page0[512 * b : 512 * (b + 1), :].rearrange("(p t) c -> p t c", t=4)[:, t, :])
 
-        wa_raw, tab, dough_t = {}, {}, {}
+        wa_raw, tab = {}, {}
         nc.sync.dma_start(idx[:], offs)
-        load_w4(0)
+        w4_raw = {}
+
+        def load_w4(b, tile):
+            w4_raw[b] = tile
+            nc.sync.dma_start(out=tile[:].bitcast(I32),
+                              in_=w4_words[:, :, H * b : H * (b + 1)].rearrange("a p c -> p a c").bitcast(I32))
+
+        load_w4(0, kept([P, KP, H], U8, "w4_raw0"))
+        load_scale_rows(tab_sc, tab_scales, (0, 2, 1, 3))
         wa_raw[0, 0] = load_wa(0, 0)
         tab[0] = load_tab(0)
+        load_scale_rows(w4_sc_raw, w4_scales, (0, 2, 1, 3))
         wa_raw[0, 1] = load_wa(0, 1)
-        tab[1] = load_tab(1)
         wa_raw[0, 2] = load_wa(0, 2)
+        tab[1] = load_tab(1)
         tab[2] = load_tab(2)
 
         wa_q, wa_s = {}, {}
         wa_bf = {}
 
         def round_wa(b, a):
-            wa_bf[b, a] = rounded(2048)
+            wa_bf[b, a] = rounded(2048) if (b, a) != (1, KP - 1) else staged([P, 2048], BF16, "last_wa_slot", 1)
             nc.scalar.copy(out=wa_bf[b, a][:].rearrange("p (t m j) -> p m j t", t=4, j=4),
                            in_=wa_raw[b, a][:].rearrange("p j (m t) -> p m j t", t=4))
 
@@ -130,75 +119,75 @@ def tile_list_pasta_crack_page_kernel(tc, tab_words, tab_scales, offs, wa, w4_wo
             nc.vector.tensor_copy(v_q[a][:], tab[a][:].bitcast(U32).indirect(idx[:]))
 
         def gather_scales():
-            v_s[0] = kept([P, S], U8, "v_s0")
-            nc.vector.tensor_copy(v_s[0][:], tab_sc[:].indirect(idx[:]))
-            for a in range(1, KP):
-                v_s[a] = shifted(v_s[0], 4 * a, "v_s%d" % a)
+            for a in range(KP):
+                v_s[a] = kept([P, S], U8, "v_s%d" % a)
+                nc.vector.tensor_copy(v_s[a][:], tab_sc[:, a, :].indirect(idx[:]))
 
-        w4_s = {}
-
-        def deal_w4_scales(b):
-            w4_s[b] = kept([P, KP, 512], U8, "w4_s%d" % b)
-            nc.vector.tensor_copy(out=w4_s[b][:].rearrange("p a (t m) -> p a t m", t=4),
-                                  in_=w4_sc_raw[:, :, 512 * b : 512 * (b + 1)].rearrange("p a (m t) -> p a t m", t=4))
-
-        w4_q = {}
+        w4_dealt = {}
 
         def deal_w4(b):
-            w4_q[b] = kept([P, KP, 1024], U8, "w4_q%d" % b)
-            nc.vector.tensor_copy(out=w4_q[b][:].bitcast(U16).rearrange("p a (t m) -> p a t m", t=4),
+            w4_dealt[b] = staged([P, KP, 1536], U8, "first_w4_slot", 1) if b == 0 else staged([P, KP, 1536], U8, "last_tab_slot", 1)
+            nc.vector.tensor_copy(out=w4_dealt[b][:, :, 0:1024].bitcast(U16).rearrange("p a (t m) -> p a t m", t=4),
                                   in_=w4_raw[b][:].bitcast(U16).rearrange("p a (m t) -> p a t m", t=4))
 
+        def deal_w4_scales(b):
+            nc.vector.tensor_copy(out=w4_dealt[b][:, :, 1024:1536].rearrange("p a (t m) -> p a t m", t=4),
+                                  in_=w4_sc_raw[:, :, 512 * b : 512 * (b + 1)].rearrange("p a (m t) -> p a t m", t=4))
+
         round_wa(0, 0)
-        deal_w4(0)
         gather_scales()
+        deal_w4(0)
         w8_sc_raw = keep.tile([P, H], U8, name="w8_sc_raw", tag="scale_rows", align_bytes=64)
         nc.gpsimd.memset(w8_sc_raw[:].bitcast(I32), 0)
-        load_scale_rows(w8_sc_raw, w8_scales)
         gather_words(0)
         round_wa(0, 1)
         quantise_wa(0, 0)
         deal_w4_scales(0)
-        gather_words(1)
         round_wa(0, 2)
         quantise_wa(0, 1)
         quantise_wa(0, 2)
+        gather_words(1)
         gather_words(2)
 
-        load_w4(1)
+        load_w4(1, staged([P, KP, H], U8, "tab_slot"))
         dough_rows = dough.rearrange("(b p t) s -> b p t s", b=HB, t=4)
-        dough_first = kept([P, S], F32, "dough_first")
-        nc.sync.dma_start(out=dough_first[:], in_=dough_rows[0, :, 0, :])
+        rows_a = kept([P, 5, S], F32, "rows_a")
+        nc.sync.dma_start(out=rows_a[:, 0, :], in_=dough_rows[0, :, 0, :])
         wgs_rows = wgs.rearrange("(v t) s -> v t s", t=4)
-        wg_first = kept([P, S], F32, "wg_first")
+        wg_first = keep.tile([P, S], F32, name="wg_first", tag="wg_first", align_bytes=64)
         for u in range(4):
             nc.sync.dma_start(out=wg_first[32 * u : 32 * (u + 1)], in_=wgs_rows[:, 0, :])
         nc.sync.dma_start(idx2[:], offs2)
-        load_page(0, 0)
+        load_page(0, 0, kept([P, T2], F32, "page00"))
         nc.sync.dma_start(idx3[:], offs3)
-        dough_rest = staged([P, 3, S], F32)
-        nc.sync.dma_start(out=dough_rest[:], in_=dough_rows[0, :, 1:4, :])
+        nc.sync.dma_start(out=rows_a[:, 1:4, :], in_=dough_rows[0, :, 1:4, :])
         wg_rest = keep.tile([P, 3, S], F32, name="wg_rest", tag="late", align_bytes=64)
         for u in range(4):
             nc.sync.dma_start(out=wg_rest[32 * u : 32 * (u + 1)], in_=wgs_rows[:, 1:4, :])
-        load_page(0, 1)
-        wa_raw[1, 0] = load_wa(1, 0)
-        load_page(0, 2)
-        wa_raw[1, 1] = load_wa(1, 1)
-        load_page(0, 3)
-        wa_raw[1, 2] = load_wa(1, 2)
-        dough_t[1] = load_rows4(dough, 1)
-        for t in range(4):
-            load_page(1, t)
-        w8_raw = staged([P, HB, H], I32)
-        nc.sync.dma_start(out=w8_raw[:], in_=w8_words.rearrange("a p c i -> p a (c i)").bitcast(I32))
+        load_page(0, 1, kept([P, T2], F32, "page01"))
+        for a in range(KP):
+            wa_raw[1, a] = load_wa(1, a)
+        load_page(0, 2, staged([P, T2], F32, "tab_slot"))
+        load_page(0, 3, staged([P, T2], F32, "tab_slot"))
+        nc.sync.dma_start(out=rows_a[:, 4, :], in_=dough_rows[1, :, 0, :])
         floor_t = kept([P, HB, 4], F32, "floor_t")
         gain_t = kept([P, HB, 4], F32, "gain_t")
         nc.sync.dma_start(out=floor_t[:], in_=floor_v.rearrange("(b p t) -> p b t", b=HB, t=4))
         nc.sync.dma_start(out=gain_t[:], in_=gain.rearrange("(b p t) -> p b t", b=HB, t=4))
+
+        def load_second_half():
+            load_page(1, 0, staged([P, T2], F32, "w4_scale_slot", 1))
+            rows = staged([P, 4, S], F32, "tab_slot")
+            nc.sync.dma_start(out=rows[:, 0:3, :], in_=dough_rows[1, :, 1:4, :])
+            load_page(1, 1, kept([P, T2], F32, "page11"))
+            load_page(1, 2, staged([P, T2], F32, "wa_slot"))
+            load_page(1, 3, staged([P, T2], F32, "wa_slot"))
+            return rows
+
         lim_t = {}
-        for mh in range(2):
-            lim_t[mh] = staged([P, 4, NX], F32)
+
+        def load_lim(mh):
+            lim_t[mh] = staged([P, 4, NX], F32, "first_w4_slot" if mh == 0 else "last_tab_slot", 1)
             nc.sync.dma_start(out=lim_t[mh][:], in_=lim[512 * mh : 512 * (mh + 1), :].rearrange("(g p) j -> p g j", p=P))
 
         tiles = [(b, t) for b in range(HB) for t in range(4)]
@@ -209,8 +198,8 @@ def tile_list_pasta_crack_page_kernel(tc, tab_words, tab_scales, offs, wa, w4_wo
             slow = bank(S)
             fast = bank(S)
             for a in range(KP):
-                nc.tensor.matmul_mx(out=slow[:], lhsT=w4_q[b][:, a, 256 * t : 256 * (t + 1)].bitcast(FP4X4),
-                                    lhsT_scale=w4_s[b][:, a, P * t : P * (t + 1)],
+                nc.tensor.matmul_mx(out=slow[:], lhsT=w4_dealt[b][:, a, 256 * t : 256 * (t + 1)].bitcast(FP4X4),
+                                    lhsT_scale=w4_dealt[b][:, a, 1024 + P * t : 1024 + P * (t + 1)],
                                     rhs=v_q[a][:].bitcast(FP8X4), rhs_scale=v_s[a][:], start=(a == 0), stop=(a == KP - 1))
                 nc.tensor.matmul_mx(out=fast[:], lhsT=wa_q[b, a][:, P * t : P * (t + 1)].bitcast(FP8X4),
                                     lhsT_scale=wa_s[b, a][:, P * t : P * (t + 1)],
@@ -223,10 +212,9 @@ def tile_list_pasta_crack_page_kernel(tc, tab_words, tab_scales, offs, wa, w4_wo
 
         def times_dough(i):
             b, t = tiles[i]
-            crack[i] = work.tile([P, S], F32, name="crack")
-            rows = dough_t[1][:, t, :] if b == 1 else dough_rest[:, t - 1, :] if t > 0 else dough_first[:]
-            engine = nc.vector if i == 0 else nc.gpsimd
-            engine.tensor_tensor(crack[i][:], top[i][:], rows, ALU.mult)
+            crack[i] = work.tile([P, S], F32, name="crack") if i != 3 else staged([P, S], F32, "last_wa_slot", 1)
+            rows = rows_a[:, i, :] if i <= 4 else rows_b[:, i - 5, :]
+            nc.vector.tensor_tensor(crack[i][:], top[i][:], rows, ALU.mult)
 
         planes = {}
 
@@ -240,16 +228,15 @@ def tile_list_pasta_crack_page_kernel(tc, tab_words, tab_scales, offs, wa, w4_wo
                 planes[b] = work.tile([P, 4, T2], BF16, name="planes", bufs=1)
             nc.scalar.copy(out=planes[b][:, t, :], in_=page[b, t][:])
 
-        x_whole = kept([P, 4, NX], F32, "x_whole")
-        x = {(0, c): x_whole[:, :, c * CW : (c + 1) * CW] for c in range(NC)}
-        for c in range(NC):
-            x[1, c] = kept([P, 4, CW], F32, "x1%d" % c)[:]
+        x = {}
 
-        def fetch_whole(t):
-            nc.vector.tensor_copy(x_whole[:, t, :], page[0, t][:].indirect(idx3[:]))
+        def fetch(i):
+            b, t = tiles[i]
+            rows = rows_a[:, i + 1, :] if b == 0 else rows_b[:, t, :]
+            nc.vector.tensor_copy(rows, page[b, t][:].indirect(idx3[:]))
 
-        def fetch(t, c):
-            nc.vector.tensor_copy(x[1, c][:, t, :], page[1, t][:].indirect(idx3[:, c * CW // 16 : (c + 1) * CW // 16]))
+        def fetch_last(c):
+            nc.vector.tensor_copy(x[1, c][:, 3, :], page[1, 3][:].indirect(idx3[:, c * CW // 16 : (c + 1) * CW // 16]))
 
         x_bf, x_q, x_s = {}, {}, {}
 
@@ -275,43 +262,48 @@ def tile_list_pasta_crack_page_kernel(tc, tab_words, tab_scales, offs, wa, w4_wo
         def quantise_page(b, mh):
             page_q[b, mh], page_s[b, mh] = quantise(page_bf[b, mh], 512, "page%d%d" % (b, mh))
 
-        w8_s = kept([P, H], U8, "w8_s")
 
         def deal_w8(b):
             cols = slice(512 * b, 512 * (b + 1))
             nc.vector.tensor_copy(out=w8_q[:, :, cols].rearrange("p a (t m) -> p a m t", t=4),
                                   in_=w8_raw[:, :, cols].bitcast(U32).rearrange("p a (m t) -> p a m t", t=4))
 
-        deal_w4(1)
-        deal_w4_scales(1)
-        nc.vector.tensor_copy(out=w8_s[:].rearrange("p (b t m) -> p b t m", b=HB, t=4),
-                              in_=w8_sc_raw[:].rearrange("p (b m t) -> p b t m", b=HB, t=4))
         readings(0)
         readings(1)
         times_dough(0)
+        deal_w4(1)
+        deal_w4_scales(1)
+        readings(2)
+        rows_b = load_second_half()
+        for c in range(NC):
+            x[0, c] = rows_a[:, 1:5, c * CW : (c + 1) * CW]
+            x[1, c] = rows_b[:, :, c * CW : (c + 1) * CW]
+        w8_raw = staged([P, HB, H], I32, "wa_slot")
+        nc.sync.dma_start(out=w8_raw[:], in_=w8_words.rearrange("a p c i -> p a (c i)").bitcast(I32))
+        for q in range(4):
+            nc.sync.dma_start(out=w8_sc_raw[32 * q : 32 * q + 8, :].bitcast(I32), in_=w8_scales[:, 4 * q : 4 * q + 4, :].bitcast(I32))
         for i in range(8):
             put(i)
-            if i < 3:
-                round_wa(1, i)
-            if i + 1 < 8:
-                times_dough(i + 1)
-            if i + 2 < 8:
-                if i == 2:
-                    quantise_wa(1, 2)
+            if i == 0:
+                readings(3)
+                load_lim(0)
+                for a in range(KP):
+                    round_wa(1, a)
+            if i == 2:
+                for a in range(KP):
+                    quantise_wa(1, a)
+            if 2 <= i <= 5:
                 readings(i + 2)
-            if i < 4:
-                fetch_whole(i)
-            else:
-                fetch(i - 4, 0)
-                if i == 7:
-                    round_x(1, 0)
-                fetch(i - 4, 1)
-                if i == 7:
-                    round_x(1, 1)
-            if i < 2:
-                quantise_wa(1, i)
+            if i == 5:
+                load_lim(1)
             if i < 7:
+                times_dough(i + 1)
+                fetch(i)
                 round_page_row(i)
+            else:
+                for c in range(NC):
+                    fetch_last(c)
+                    round_x(1, c)
             if i == 3:
                 round_x(0, 0)
                 round_x(0, 1)
@@ -323,6 +315,9 @@ def tile_list_pasta_crack_page_kernel(tc, tab_words, tab_scales, offs, wa, w4_wo
                 quantise_page(0, 0)
                 weave_page(0, 1, 4)
             if i == 6:
+                w8_s = keep.tile([P, H], U8, name="w8_s", tag="wg_first", align_bytes=64)
+                nc.vector.tensor_copy(out=w8_s[:].rearrange("p (b t m) -> p b t m", b=HB, t=4),
+                                      in_=w8_sc_raw[:].rearrange("p (b m t) -> p b t m", b=HB, t=4))
                 quantise_page(0, 1)
                 weave_page(1, 0, 3)
                 weave_page(1, 1, 3)
@@ -357,20 +352,19 @@ def tile_list_pasta_crack_page_kernel(tc, tab_words, tab_scales, offs, wa, w4_wo
         def quantise_z(b, c):
             z_q[b, c], z_s[b, c] = quantise(z_bf[b, c], CW, "z%d%d" % (b, c))
 
-        def score(c, mh):
+        def score(c, mh, g0, count):
             cols = slice(c * CW, (c + 1) * CW)
-            for g0 in (0, 2):
-                e = psum.tile([P, 2, CW], F32, name="bank")
-                for g in (g0, g0 + 1):
-                    for b in range(HB):
-                        nc.tensor.matmul_mx(out=e[:, g - g0, :], lhsT=page_q[b, mh][:, P * g : P * (g + 1)].bitcast(FP8X4),
-                                            lhsT_scale=page_s[b, mh][:, P * g : P * (g + 1)],
-                                            rhs=z_q[b, c][:].bitcast(FP8X4), rhs_scale=z_s[b, c][:], start=(b == 0), stop=(b == HB - 1))
-                result = lim_t[mh][:, g0 : g0 + 2, cols]
-                nc.vector.tensor_tensor(result, e[:], result, ALU.min)
-                nc.scalar.activation(result, result, ACT.Abs)
-                row = 512 * mh + P * g0
-                nc.sync.dma_start(out=out[row : row + 2 * P, cols].rearrange("(g p) j -> p g j", p=P), in_=result)
+            e = psum.tile([P, count, CW], F32, name="bank")
+            for g in range(g0, g0 + count):
+                for b in range(HB):
+                    nc.tensor.matmul_mx(out=e[:, g - g0, :], lhsT=page_q[b, mh][:, P * g : P * (g + 1)].bitcast(FP8X4),
+                                        lhsT_scale=page_s[b, mh][:, P * g : P * (g + 1)],
+                                        rhs=z_q[b, c][:].bitcast(FP8X4), rhs_scale=z_s[b, c][:], start=(b == 0), stop=(b == HB - 1))
+            result = lim_t[mh][:, g0 : g0 + count, cols]
+            nc.vector.tensor_tensor(result, e[:], result, ALU.min)
+            nc.scalar.activation(result, result, ACT.Abs)
+            row = 512 * mh + P * g0
+            nc.sync.dma_start(out=out[row : row + count * P, cols].rearrange("(g p) j -> p g j", p=P), in_=result)
 
         deal_w8(0)
         quantise_x(1, 0)
@@ -388,11 +382,16 @@ def tile_list_pasta_crack_page_kernel(tc, tab_words, tab_scales, offs, wa, w4_wo
         quantise_z(1, 0)
         quantise_page(1, 0)
         lift(1, 1)
-        round_z(1, 1)
-        score(0, 0)
+        round_z_on_scalar(1, 1)
+        score(0, 0, 0, 2)
         quantise_page(1, 1)
+        score(0, 0, 2, 2)
         quantise_z(0, 1)
+        score(0, 1, 0, 2)
         quantise_z(1, 1)
-        score(0, 1)
-        score(1, 0)
-        score(1, 1)
+        score(0, 1, 2, 2)
+        score(1, 0, 0, 2)
+        score(1, 0, 2, 2)
+        score(1, 1, 0, 2)
+        score(1, 1, 2, 1)
+        score(1, 1, 3, 1)

@@ -17,10 +17,14 @@ ALU = mybir.AluOpType
 ACT = mybir.ActivationFunctionType
 
 P = 128
-KP = K // 512
-HB = H // 512
+PACK = 4
+PASS = P * PACK
+K_PASSES = K // PASS
+H_PASSES = H // PASS
 CW = 256
-NC = NX // CW
+CHUNKS = NX // CW
+W4_BYTES = 2 * PASS
+QUADRANT_ORDER = (0, 2, 1, 3)
 
 
 def tile_list_pasta_crack_page_kernel(tc, tab_words, tab_scales, offs, wa, w4_words, w4_scales, dough, wgs,
@@ -49,59 +53,55 @@ def tile_list_pasta_crack_page_kernel(tc, tab_words, tab_scales, offs, wa, w4_wo
         idx2 = kept([P, S // 16], U16, "idx2")
         idx3 = kept([P, NX // 16], U16, "idx3")
 
-        tab_sc = keep.tile([P, KP, T], U8, name="tab_sc", tag="scale_rows", align_bytes=64)
-        w4_sc_raw = staged([P, KP, H], U8, "w4_scale_slot", 1)
+        tab_sc = keep.tile([P, K_PASSES, T], U8, name="tab_sc", tag="scale_rows", align_bytes=64)
+        w4_sc_raw = staged([P, K_PASSES, H], U8, "w4_scale_slot", 1)
         nc.gpsimd.memset(tab_sc[:, 0, :].bitcast(I32), 0)
-        nc.vector.memset(tab_sc[:, 1:KP, :].rearrange("p a c -> p (a c)").bitcast(I32), 0)
+        nc.vector.memset(tab_sc[:, 1:K_PASSES, :].rearrange("p a c -> p (a c)").bitcast(I32), 0)
         nc.gpsimd.memset(w4_sc_raw[:].rearrange("p a c -> p (a c)").bitcast(I32), 0)
 
-        def load_scale_rows(dst, src, quadrants):
-            for q in quadrants:
+        def load_scale_rows(dst, src):
+            for q in QUADRANT_ORDER:
                 nc.sync.dma_start(out=dst[32 * q : 32 * q + 4].bitcast(I32),
-                                in_=src[:, 4 * q : 4 * q + 4, :].rearrange("a r c -> r a c").bitcast(I32))
+                                  in_=src[:, 4 * q : 4 * q + 4, :].rearrange("a r c -> r a c").bitcast(I32))
+
+        wa_raw, tab, w4_raw, page = {}, {}, {}, {}
 
         def load_wa(b, a):
-            raw = staged([P, 4, 512], F32, "wa_slot")
-            nc.sync.dma_start(out=raw[:], in_=wa[512 * a : 512 * (a + 1), 512 * b : 512 * (b + 1)].rearrange("(p j) c -> p j c", j=4))
-            return raw
+            wa_raw[b, a] = staged([P, PACK, PASS], F32, "wa_slot")
+            rows = wa[PASS * a : PASS * (a + 1), PASS * b : PASS * (b + 1)]
+            nc.sync.dma_start(out=wa_raw[b, a][:], in_=rows.rearrange("(p j) c -> p j c", j=PACK))
 
-        def load_tab(a):
-            words = staged([P, T], I32, "tab_slot") if a < KP - 1 else staged([P, T], I32, "last_tab_slot", 1)
-            nc.sync.dma_start(out=words[:], in_=tab_words[a].rearrange("p t i -> p (t i)").bitcast(I32))
-            return words
-
-        page = {}
-
-        def load_page(b, t, tile):
-            page[b, t] = tile
-            nc.sync.dma_start(out=tile[:], in_=page0[512 * b : 512 * (b + 1), :].rearrange("(p t) c -> p t c", t=4)[:, t, :])
-
-        wa_raw, tab = {}, {}
-        nc.sync.dma_start(idx[:], offs)
-        w4_raw = {}
+        def load_tab(a, tile):
+            tab[a] = tile
+            nc.sync.dma_start(out=tile[:], in_=tab_words[a].rearrange("p t i -> p (t i)").bitcast(I32))
 
         def load_w4(b, tile):
             w4_raw[b] = tile
-            nc.sync.dma_start(out=tile[:].bitcast(I32),
-                              in_=w4_words[:, :, H * b : H * (b + 1)].rearrange("a p c -> p a c").bitcast(I32))
+            columns = w4_words[:, :, W4_BYTES * b : W4_BYTES * (b + 1)]
+            nc.sync.dma_start(out=tile[:].bitcast(I32), in_=columns.rearrange("a p c -> p a c").bitcast(I32))
 
-        load_w4(0, kept([P, KP, H], U8, "w4_raw0"))
-        load_scale_rows(tab_sc, tab_scales, (0, 2, 1, 3))
-        wa_raw[0, 0] = load_wa(0, 0)
-        tab[0] = load_tab(0)
-        load_scale_rows(w4_sc_raw, w4_scales, (0, 2, 1, 3))
-        wa_raw[0, 1] = load_wa(0, 1)
-        wa_raw[0, 2] = load_wa(0, 2)
-        tab[1] = load_tab(1)
-        tab[2] = load_tab(2)
+        def load_page(b, t, tile):
+            page[b, t] = tile
+            rows = page0[PASS * b : PASS * (b + 1), :].rearrange("(p t) c -> p t c", t=PACK)
+            nc.sync.dma_start(out=tile[:], in_=rows[:, t, :])
 
-        wa_q, wa_s = {}, {}
-        wa_bf = {}
+        nc.sync.dma_start(idx[:], offs)
+        load_w4(0, kept([P, K_PASSES, W4_BYTES], U8, "w4_raw0"))
+        load_scale_rows(tab_sc, tab_scales)
+        load_wa(0, 0)
+        load_tab(0, staged([P, T], I32, "tab_slot"))
+        load_scale_rows(w4_sc_raw, w4_scales)
+        load_wa(0, 1)
+        load_wa(0, 2)
+        load_tab(1, staged([P, T], I32, "tab_slot"))
+        load_tab(2, staged([P, T], I32, "last_tab_slot", 1))
 
-        def round_wa(b, a):
-            wa_bf[b, a] = rounded(2048) if (b, a) != (1, KP - 1) else staged([P, 2048], BF16, "last_wa_slot", 1)
-            nc.scalar.copy(out=wa_bf[b, a][:].rearrange("p (t m j) -> p m j t", t=4, j=4),
-                           in_=wa_raw[b, a][:].rearrange("p j (m t) -> p m j t", t=4))
+        wa_bf, wa_q, wa_s = {}, {}, {}
+
+        def round_wa(b, a, tile):
+            wa_bf[b, a] = tile
+            nc.scalar.copy(out=tile[:].rearrange("p (t m j) -> p m j t", t=PACK, j=PACK),
+                           in_=wa_raw[b, a][:].rearrange("p j (m t) -> p m j t", t=PACK))
 
         def quantise(src, cols, name):
             codes = kept([P, cols], U32, name + "_q")
@@ -110,7 +110,7 @@ def tile_list_pasta_crack_page_kernel(tc, tab_words, tab_scales, offs, wa, w4_wo
             return codes, scales
 
         def quantise_wa(b, a):
-            wa_q[b, a], wa_s[b, a] = quantise(wa_bf[b, a], 512, "wa%d%d" % (b, a))
+            wa_q[b, a], wa_s[b, a] = quantise(wa_bf[b, a], PASS, "wa%d%d" % (b, a))
 
         v_q, v_s = {}, {}
 
@@ -118,236 +118,267 @@ def tile_list_pasta_crack_page_kernel(tc, tab_words, tab_scales, offs, wa, w4_wo
             v_q[a] = kept([P, S], U32, "v_q%d" % a)
             nc.vector.tensor_copy(v_q[a][:], tab[a][:].bitcast(U32).indirect(idx[:]))
 
-        def gather_scales():
-            for a in range(KP):
-                v_s[a] = kept([P, S], U8, "v_s%d" % a)
-                nc.vector.tensor_copy(v_s[a][:], tab_sc[:, a, :].indirect(idx[:]))
+        def gather_scales(a):
+            v_s[a] = kept([P, S], U8, "v_s%d" % a)
+            nc.vector.tensor_copy(v_s[a][:], tab_sc[:, a, :].indirect(idx[:]))
 
         w4_dealt = {}
 
-        def deal_w4(b):
-            w4_dealt[b] = staged([P, KP, 1536], U8, "first_w4_slot", 1) if b == 0 else staged([P, KP, 1536], U8, "last_tab_slot", 1)
-            nc.vector.tensor_copy(out=w4_dealt[b][:, :, 0:1024].bitcast(U16).rearrange("p a (t m) -> p a t m", t=4),
-                                  in_=w4_raw[b][:].bitcast(U16).rearrange("p a (m t) -> p a t m", t=4))
+        def deal_w4(b, tag):
+            w4_dealt[b] = staged([P, K_PASSES, W4_BYTES + PASS], U8, tag, 1)
+            nc.vector.tensor_copy(out=w4_dealt[b][:, :, 0:W4_BYTES].bitcast(U16).rearrange("p a (t m) -> p a t m", t=PACK),
+                                  in_=w4_raw[b][:].bitcast(U16).rearrange("p a (m t) -> p a t m", t=PACK))
 
         def deal_w4_scales(b):
-            nc.vector.tensor_copy(out=w4_dealt[b][:, :, 1024:1536].rearrange("p a (t m) -> p a t m", t=4),
-                                  in_=w4_sc_raw[:, :, 512 * b : 512 * (b + 1)].rearrange("p a (m t) -> p a t m", t=4))
+            nc.vector.tensor_copy(out=w4_dealt[b][:, :, W4_BYTES : W4_BYTES + PASS].rearrange("p a (t m) -> p a t m", t=PACK),
+                                  in_=w4_sc_raw[:, :, PASS * b : PASS * (b + 1)].rearrange("p a (m t) -> p a t m", t=PACK))
 
-        round_wa(0, 0)
-        gather_scales()
-        deal_w4(0)
+        round_wa(0, 0, rounded(PACK * PASS))
+        for a in range(K_PASSES):
+            gather_scales(a)
+        deal_w4(0, "first_w4_slot")
         w8_sc_raw = keep.tile([P, H], U8, name="w8_sc_raw", tag="scale_rows", align_bytes=64)
         nc.gpsimd.memset(w8_sc_raw[:].bitcast(I32), 0)
         gather_words(0)
-        round_wa(0, 1)
+        round_wa(0, 1, rounded(PACK * PASS))
         quantise_wa(0, 0)
         deal_w4_scales(0)
-        round_wa(0, 2)
+        round_wa(0, 2, rounded(PACK * PASS))
         quantise_wa(0, 1)
         quantise_wa(0, 2)
         gather_words(1)
         gather_words(2)
 
-        load_w4(1, staged([P, KP, H], U8, "tab_slot"))
-        dough_rows = dough.rearrange("(b p t) s -> b p t s", b=HB, t=4)
-        rows_a = kept([P, 5, S], F32, "rows_a")
-        nc.sync.dma_start(out=rows_a[:, 0, :], in_=dough_rows[0, :, 0, :])
-        wgs_rows = wgs.rearrange("(v t) s -> v t s", t=4)
+        load_w4(1, staged([P, K_PASSES, W4_BYTES], U8, "tab_slot"))
+        dough_rows = dough.rearrange("(b p t) s -> b p t s", b=H_PASSES, t=PACK)
+        rows = {0: kept([P, PACK, S], F32, "rows_a")}
+        nc.sync.dma_start(out=rows[0][:, 0, :], in_=dough_rows[0, :, 0, :])
+        wgs_rows = wgs.rearrange("(v t) s -> v t s", t=PACK)
         wg_first = keep.tile([P, S], F32, name="wg_first", tag="wg_first", align_bytes=64)
-        for u in range(4):
-            nc.sync.dma_start(out=wg_first[32 * u : 32 * (u + 1)], in_=wgs_rows[:, 0, :])
+        for q in range(4):
+            nc.sync.dma_start(out=wg_first[32 * q : 32 * (q + 1)], in_=wgs_rows[:, 0, :])
         nc.sync.dma_start(idx2[:], offs2)
         load_page(0, 0, kept([P, T2], F32, "page00"))
         nc.sync.dma_start(idx3[:], offs3)
-        nc.sync.dma_start(out=rows_a[:, 1:4, :], in_=dough_rows[0, :, 1:4, :])
-        wg_rest = keep.tile([P, 3, S], F32, name="wg_rest", tag="late", align_bytes=64)
-        for u in range(4):
-            nc.sync.dma_start(out=wg_rest[32 * u : 32 * (u + 1)], in_=wgs_rows[:, 1:4, :])
+        nc.sync.dma_start(out=rows[0][:, 1:PACK, :], in_=dough_rows[0, :, 1:PACK, :])
+        wg_rest = keep.tile([P, PACK - 1, S], F32, name="wg_rest", tag="late", align_bytes=64)
+        for q in range(4):
+            nc.sync.dma_start(out=wg_rest[32 * q : 32 * (q + 1)], in_=wgs_rows[:, 1:PACK, :])
         load_page(0, 1, kept([P, T2], F32, "page01"))
-        for a in range(KP):
-            wa_raw[1, a] = load_wa(1, a)
+        for a in range(K_PASSES):
+            load_wa(1, a)
         load_page(0, 2, staged([P, T2], F32, "tab_slot"))
         load_page(0, 3, staged([P, T2], F32, "tab_slot"))
-        nc.sync.dma_start(out=rows_a[:, 4, :], in_=dough_rows[1, :, 0, :])
-        floor_t = kept([P, HB, 4], F32, "floor_t")
-        gain_t = kept([P, HB, 4], F32, "gain_t")
-        nc.sync.dma_start(out=floor_t[:], in_=floor_v.rearrange("(b p t) -> p b t", b=HB, t=4))
-        nc.sync.dma_start(out=gain_t[:], in_=gain.rearrange("(b p t) -> p b t", b=HB, t=4))
-
-        def load_second_half():
-            load_page(1, 0, staged([P, T2], F32, "w4_scale_slot", 1))
-            rows = staged([P, 4, S], F32, "tab_slot")
-            nc.sync.dma_start(out=rows[:, 0:3, :], in_=dough_rows[1, :, 1:4, :])
-            load_page(1, 1, kept([P, T2], F32, "page11"))
-            load_page(1, 2, staged([P, T2], F32, "wa_slot"))
-            load_page(1, 3, staged([P, T2], F32, "wa_slot"))
-            return rows
+        floor_t = kept([P, H_PASSES, PACK], F32, "floor_t")
+        gain_t = kept([P, H_PASSES, PACK], F32, "gain_t")
+        nc.sync.dma_start(out=floor_t[:], in_=floor_v.rearrange("(b p t) -> p b t", b=H_PASSES, t=PACK))
+        nc.sync.dma_start(out=gain_t[:], in_=gain.rearrange("(b p t) -> p b t", b=H_PASSES, t=PACK))
 
         lim_t = {}
 
-        def load_lim(mh):
-            lim_t[mh] = staged([P, 4, NX], F32, "first_w4_slot" if mh == 0 else "last_tab_slot", 1)
-            nc.sync.dma_start(out=lim_t[mh][:], in_=lim[512 * mh : 512 * (mh + 1), :].rearrange("(g p) j -> p g j", p=P))
+        def load_lim(mh, tag):
+            lim_t[mh] = staged([P, PACK, NX], F32, tag, 1)
+            nc.sync.dma_start(out=lim_t[mh][:], in_=lim[PASS * mh : PASS * (mh + 1), :].rearrange("(g p) j -> p g j", p=P))
 
-        tiles = [(b, t) for b in range(HB) for t in range(4)]
+        tiles = [(b, t) for b in range(H_PASSES) for t in range(PACK)]
+        last_tile = len(tiles) - 1
+        last_of_first_half = PACK - 1
         top, crack = {}, {}
 
         def readings(i):
             b, t = tiles[i]
             slow = bank(S)
             fast = bank(S)
-            for a in range(KP):
-                nc.tensor.matmul_mx(out=slow[:], lhsT=w4_dealt[b][:, a, 256 * t : 256 * (t + 1)].bitcast(FP4X4),
-                                    lhsT_scale=w4_dealt[b][:, a, 1024 + P * t : 1024 + P * (t + 1)],
-                                    rhs=v_q[a][:].bitcast(FP8X4), rhs_scale=v_s[a][:], start=(a == 0), stop=(a == KP - 1))
+            for a in range(K_PASSES):
+                first, last = a == 0, a == K_PASSES - 1
+                nc.tensor.matmul_mx(out=slow[:], lhsT=w4_dealt[b][:, a, 2 * P * t : 2 * P * (t + 1)].bitcast(FP4X4),
+                                    lhsT_scale=w4_dealt[b][:, a, W4_BYTES + P * t : W4_BYTES + P * (t + 1)],
+                                    rhs=v_q[a][:].bitcast(FP8X4), rhs_scale=v_s[a][:], start=first, stop=last)
                 nc.tensor.matmul_mx(out=fast[:], lhsT=wa_q[b, a][:, P * t : P * (t + 1)].bitcast(FP8X4),
                                     lhsT_scale=wa_s[b, a][:, P * t : P * (t + 1)],
-                                    rhs=v_q[a][:].bitcast(FP8X4), rhs_scale=v_s[a][:], start=(a == 0), stop=(a == KP - 1))
+                                    rhs=v_q[a][:].bitcast(FP8X4), rhs_scale=v_s[a][:], start=first, stop=last)
             slow_sb = work.tile([P, S], F32, name="slow_sb")
             nc.scalar.copy(out=slow_sb[:], in_=slow[:])
-            top[i] = work.tile([P, S], F32, name="top", bufs=3)
+            top[i] = work.tile([P, S], F32, name="top", bufs=4)
             nc.vector.tensor_tensor(top[i][:], fast[:], slow_sb[:], ALU.max)
             nc.scalar.activation(top[i][:], top[i][:], ACT.Tanh)
 
         def times_dough(i):
             b, t = tiles[i]
-            crack[i] = work.tile([P, S], F32, name="crack") if i != 3 else staged([P, S], F32, "last_wa_slot", 1)
-            rows = rows_a[:, i, :] if i <= 4 else rows_b[:, i - 5, :]
-            nc.vector.tensor_tensor(crack[i][:], top[i][:], rows, ALU.mult)
-
-        planes = {}
+            if i == last_of_first_half:
+                crack[i] = staged([P, S], F32, "last_wa_slot", 1)
+            else:
+                crack[i] = work.tile([P, S], F32, name="crack")
+            engine = nc.vector if i in (0, last_of_first_half) else nc.gpsimd
+            engine.tensor_tensor(crack[i][:], top[i][:], rows[b][:, t, :], ALU.mult)
 
         def put(i):
             b, t = tiles[i]
-            nc.vector.tensor_tensor(page[b, t][:].indirect(idx2[:]), crack[i][:], wg_rest[:, t - 1, :] if t > 0 else wg_first[:], ALU.mult)
-
-        def round_page_row(i):
-            b, t = tiles[i]
-            if t == 0:
-                planes[b] = work.tile([P, 4, T2], BF16, name="planes", bufs=1)
-            nc.scalar.copy(out=planes[b][:, t, :], in_=page[b, t][:])
+            weights = wg_rest[:, t - 1, :] if t > 0 else wg_first[:]
+            nc.vector.tensor_tensor(page[b, t][:].indirect(idx2[:]), crack[i][:], weights, ALU.mult)
 
         x = {}
 
         def fetch(i):
             b, t = tiles[i]
-            rows = rows_a[:, i + 1, :] if b == 0 else rows_b[:, t, :]
-            nc.vector.tensor_copy(rows, page[b, t][:].indirect(idx3[:]))
+            nc.vector.tensor_copy(rows[b][:, t, :], page[b, t][:].indirect(idx3[:]))
 
         def fetch_last(c):
-            nc.vector.tensor_copy(x[1, c][:, 3, :], page[1, 3][:].indirect(idx3[:, c * CW // 16 : (c + 1) * CW // 16]))
+            b, t = tiles[last_tile]
+            nc.vector.tensor_copy(x[b, c][:, t, :], page[b, t][:].indirect(idx3[:, c * CW // 16 : (c + 1) * CW // 16]))
+
+        def woven(tile):
+            return tile.rearrange("p (c i t) -> p c t i", i=4, t=PACK)
+
+        def by_rows(row_tiles):
+            return row_tiles.rearrange("p t (c i) -> p c t i", i=4)
 
         x_bf, x_q, x_s = {}, {}, {}
 
         def round_x(b, c):
-            x_bf[b, c] = rounded(4 * CW)
-            nc.scalar.copy(out=x_bf[b, c][:].rearrange("p (c i t) -> p c t i", i=4, t=4),
-                           in_=x[b, c].rearrange("p t (c i) -> p c t i", i=4))
+            x_bf[b, c] = rounded(PACK * CW)
+            nc.scalar.copy(out=woven(x_bf[b, c][:]), in_=by_rows(x[b, c]))
 
         def quantise_x(b, c):
             x_q[b, c], x_s[b, c] = quantise(x_bf[b, c], CW, "x%d%d" % (b, c))
 
-        page_bf, page_q, page_s = {}, {}, {}
+        page_rows, page_bf, page_q, page_s = {}, {}, {}, {}
 
-        def weave_page(b, mh, rows):
-            page_bf[b, mh] = rounded(2048) if b == 0 else kept([P, 2048], BF16, "page_bf%d" % mh)
-            nc.scalar.copy(out=page_bf[b, mh][:].rearrange("p (c i t) -> p c t i", i=4, t=4)[:, :, 0:rows, :],
-                           in_=planes[b][:, 0:rows, 512 * mh : 512 * (mh + 1)].rearrange("p t (c i) -> p c t i", i=4))
+        def round_page_row(i):
+            b, t = tiles[i]
+            if t == 0:
+                page_rows[b] = work.tile([P, PACK, T2], BF16, name="planes", bufs=1)
+            nc.scalar.copy(out=page_rows[b][:, t, :], in_=page[b, t][:])
+
+        def weave_page(b, mh, row_count, tile):
+            page_bf[b, mh] = tile
+            nc.scalar.copy(out=woven(tile[:])[:, :, 0:row_count, :],
+                           in_=by_rows(page_rows[b][:, 0:row_count, PASS * mh : PASS * (mh + 1)]))
 
         def weave_last_row(mh):
-            nc.scalar.copy(out=page_bf[1, mh][:].rearrange("p (m t) -> p m t", t=4)[:, :, 3],
-                           in_=page[1, 3][:, 512 * mh : 512 * (mh + 1)])
+            b, t = tiles[last_tile]
+            nc.scalar.copy(out=page_bf[b, mh][:].rearrange("p (m t) -> p m t", t=PACK)[:, :, t],
+                           in_=page[b, t][:, PASS * mh : PASS * (mh + 1)])
 
         def quantise_page(b, mh):
-            page_q[b, mh], page_s[b, mh] = quantise(page_bf[b, mh], 512, "page%d%d" % (b, mh))
-
-
-        def deal_w8(b):
-            cols = slice(512 * b, 512 * (b + 1))
-            nc.vector.tensor_copy(out=w8_q[:, :, cols].rearrange("p a (t m) -> p a m t", t=4),
-                                  in_=w8_raw[:, :, cols].bitcast(U32).rearrange("p a (m t) -> p a m t", t=4))
+            page_q[b, mh], page_s[b, mh] = quantise(page_bf[b, mh], PASS, "page%d%d" % (b, mh))
 
         readings(0)
         readings(1)
         times_dough(0)
-        deal_w4(1)
+        deal_w4(1, "last_tab_slot")
         deal_w4_scales(1)
         readings(2)
-        rows_b = load_second_half()
-        for c in range(NC):
-            x[0, c] = rows_a[:, 1:5, c * CW : (c + 1) * CW]
-            x[1, c] = rows_b[:, :, c * CW : (c + 1) * CW]
-        w8_raw = staged([P, HB, H], I32, "wa_slot")
+
+        load_page(1, 0, staged([P, T2], F32, "w4_scale_slot", 1))
+        rows[1] = staged([P, PACK, S], F32, "tab_slot")
+        nc.sync.dma_start(out=rows[1][:], in_=dough_rows[1])
+        load_page(1, 1, kept([P, T2], F32, "page11"))
+        load_page(1, 2, staged([P, T2], F32, "wa_slot"))
+        load_page(1, 3, staged([P, T2], F32, "wa_slot"))
+        for b in range(H_PASSES):
+            for c in range(CHUNKS):
+                x[b, c] = rows[b][:, :, c * CW : (c + 1) * CW]
+        w8_raw = staged([P, H_PASSES, H], I32, "wa_slot")
         nc.sync.dma_start(out=w8_raw[:], in_=w8_words.rearrange("a p c i -> p a (c i)").bitcast(I32))
         for q in range(4):
-            nc.sync.dma_start(out=w8_sc_raw[32 * q : 32 * q + 8, :].bitcast(I32), in_=w8_scales[:, 4 * q : 4 * q + 4, :].bitcast(I32))
-        for i in range(8):
-            put(i)
-            if i == 0:
-                readings(3)
-                load_lim(0)
-                for a in range(KP):
-                    round_wa(1, a)
-            if i == 2:
-                for a in range(KP):
-                    quantise_wa(1, a)
-            if 2 <= i <= 5:
-                readings(i + 2)
-            if i == 5:
-                load_lim(1)
-            if i < 7:
-                times_dough(i + 1)
-                fetch(i)
-                round_page_row(i)
-            else:
-                for c in range(NC):
-                    fetch_last(c)
-                    round_x(1, c)
-            if i == 3:
-                round_x(0, 0)
-                round_x(0, 1)
-            if i == 4:
-                quantise_x(0, 0)
-                quantise_x(0, 1)
-                weave_page(0, 0, 4)
-            if i == 5:
-                quantise_page(0, 0)
-                weave_page(0, 1, 4)
-            if i == 6:
-                w8_s = keep.tile([P, H], U8, name="w8_s", tag="wg_first", align_bytes=64)
-                nc.vector.tensor_copy(out=w8_s[:].rearrange("p (b t m) -> p b t m", b=HB, t=4),
-                                      in_=w8_sc_raw[:].rearrange("p (b m t) -> p b t m", b=HB, t=4))
-                quantise_page(0, 1)
-                weave_page(1, 0, 3)
-                weave_page(1, 1, 3)
-        w8_q = keep.tile([P, HB, H], U32, name="w8_q", tag="late", align_bytes=64)
+            nc.sync.dma_start(out=w8_sc_raw[32 * q : 32 * q + 4 * H_PASSES, :].bitcast(I32),
+                              in_=w8_scales[:, 4 * q : 4 * q + 4, :].bitcast(I32))
+
+        def finish_tile(i):
+            fetch(i)
+            round_page_row(i)
+
+        put(0)
+        readings(3)
+        load_lim(0, "first_w4_slot")
+        for a in range(K_PASSES - 1):
+            round_wa(1, a, rounded(PACK * PASS))
+        round_wa(1, K_PASSES - 1, staged([P, PACK * PASS], BF16, "last_wa_slot", 1))
+        times_dough(1)
+        finish_tile(0)
+
+        put(1)
+        times_dough(2)
+        finish_tile(1)
+
+        put(2)
+        for a in range(K_PASSES):
+            quantise_wa(1, a)
+        times_dough(3)
+        readings(4)
+        readings(5)
+        finish_tile(2)
+
+        put(3)
+        times_dough(4)
+        readings(6)
+        readings(7)
+        load_lim(1, "last_tab_slot")
+        finish_tile(3)
+        for c in range(CHUNKS):
+            round_x(0, c)
+
+        put(4)
+        times_dough(5)
+        finish_tile(4)
+        for c in range(CHUNKS):
+            quantise_x(0, c)
+        weave_page(0, 0, PACK, rounded(PACK * PASS))
+
+        put(5)
+        times_dough(6)
+        finish_tile(5)
+        quantise_page(0, 0)
+        weave_page(0, 1, PACK, rounded(PACK * PASS))
+
+        put(6)
+        times_dough(7)
+        finish_tile(6)
+        w8_s = keep.tile([P, H], U8, name="w8_s", tag="wg_first", align_bytes=64)
+        nc.vector.tensor_copy(out=w8_s[:].rearrange("p (b t m) -> p b t m", b=H_PASSES, t=PACK),
+                              in_=w8_sc_raw[:].rearrange("p (b m t) -> p b t m", b=H_PASSES, t=PACK))
+        quantise_page(0, 1)
+        for mh in range(T2 // PASS):
+            weave_page(1, mh, PACK - 1, kept([P, PACK * PASS], BF16, "page_bf%d" % mh))
+
+        put(last_tile)
+        for c in range(CHUNKS):
+            fetch_last(c)
+            round_x(1, c)
+
+        w8_q = keep.tile([P, H_PASSES, H], U32, name="w8_q", tag="late", align_bytes=64)
+
+        def deal_w8(b):
+            cols = slice(PASS * b, PASS * (b + 1))
+            nc.vector.tensor_copy(out=w8_q[:, :, cols].rearrange("p a (t m) -> p a m t", t=PACK),
+                                  in_=w8_raw[:, :, cols].bitcast(U32).rearrange("p a (m t) -> p a m t", t=PACK))
+
+        def lift(b, c):
+            for t in range(PACK):
+                y = bank(CW)
+                col = PASS * b + P * t
+                for a in range(H_PASSES):
+                    nc.tensor.matmul_mx(out=y[:], lhsT=w8_q[:, a, col : col + P].bitcast(FP8X4),
+                                        lhsT_scale=w8_s[4 * a : P, col : col + P],
+                                        rhs=x_q[a, c][:].bitcast(FP8X4), rhs_scale=x_s[a, c][:],
+                                        start=(a == 0), stop=(a == H_PASSES - 1))
+                nc.vector.scalar_tensor_tensor(x[b, c][:, t, :], y[:], floor_t[:, b, t : t + 1], x[b, c][:, t, :],
+                                               ALU.max, ALU.add)
 
         z_bf, z_q, z_s = {}, {}, {}
 
-        def lift(b, c):
-            for t in range(4):
-                y = bank(CW)
-                col = 512 * b + P * t
-                for a in range(HB):
-                    nc.tensor.matmul_mx(out=y[:], lhsT=w8_q[:, a, col : col + P].bitcast(FP8X4),
-                                        lhsT_scale=w8_s[4 * a : P, col : col + P],
-                                        rhs=x_q[a, c][:].bitcast(FP8X4), rhs_scale=x_s[a, c][:], start=(a == 0), stop=(a == HB - 1))
-                nc.vector.scalar_tensor_tensor(x[b, c][:, t, :], y[:], floor_t[:, b, t : t + 1], x[b, c][:, t, :], ALU.max, ALU.add)
-
-        def round_z(b, c):
-            z_bf[b, c] = rounded(4 * CW)
-            nc.vector.tensor_tensor(z_bf[b, c][:].rearrange("p (c i t) -> p c t i", i=4, t=4),
-                                    x[b, c].rearrange("p t (c i) -> p c t i", i=4),
-                                    gain_t[:, b, :].unsqueeze(1).unsqueeze(3).to_broadcast([P, CW // 4, 4, 4]), ALU.mult)
+        def round_z_on_vector(b, c):
+            z_bf[b, c] = rounded(PACK * CW)
+            gains = gain_t[:, b, :].unsqueeze(1).unsqueeze(3).to_broadcast([P, CW // 4, PACK, 4])
+            nc.vector.tensor_tensor(woven(z_bf[b, c][:]), by_rows(x[b, c]), gains, ALU.mult)
 
         def round_z_on_scalar(b, c):
-            z_rows = work.tile([P, 4, CW], BF16, name="z_rows")
-            for t in range(4):
+            z_rows = work.tile([P, PACK, CW], BF16, name="z_rows")
+            for t in range(PACK):
                 nc.scalar.activation(z_rows[:, t, :], x[b, c][:, t, :], ACT.Copy, scale=gain_t[:, b, t : t + 1])
-            z_bf[b, c] = rounded(4 * CW)
-            nc.scalar.copy(out=z_bf[b, c][:].rearrange("p (c i t) -> p c t i", i=4, t=4),
-                           in_=z_rows[:].rearrange("p t (c i) -> p c t i", i=4))
+            z_bf[b, c] = rounded(PACK * CW)
+            nc.scalar.copy(out=woven(z_bf[b, c][:]), in_=by_rows(z_rows[:]))
 
         def quantise_z(b, c):
             z_q[b, c], z_s[b, c] = quantise(z_bf[b, c], CW, "z%d%d" % (b, c))
@@ -356,14 +387,15 @@ def tile_list_pasta_crack_page_kernel(tc, tab_words, tab_scales, offs, wa, w4_wo
             cols = slice(c * CW, (c + 1) * CW)
             e = psum.tile([P, count, CW], F32, name="bank")
             for g in range(g0, g0 + count):
-                for b in range(HB):
+                for b in range(H_PASSES):
                     nc.tensor.matmul_mx(out=e[:, g - g0, :], lhsT=page_q[b, mh][:, P * g : P * (g + 1)].bitcast(FP8X4),
                                         lhsT_scale=page_s[b, mh][:, P * g : P * (g + 1)],
-                                        rhs=z_q[b, c][:].bitcast(FP8X4), rhs_scale=z_s[b, c][:], start=(b == 0), stop=(b == HB - 1))
+                                        rhs=z_q[b, c][:].bitcast(FP8X4), rhs_scale=z_s[b, c][:],
+                                        start=(b == 0), stop=(b == H_PASSES - 1))
             result = lim_t[mh][:, g0 : g0 + count, cols]
             nc.vector.tensor_tensor(result, e[:], result, ALU.min)
             nc.scalar.activation(result, result, ACT.Abs)
-            row = 512 * mh + P * g0
+            row = PASS * mh + P * g0
             nc.sync.dma_start(out=out[row : row + count * P, cols].rearrange("(g p) j -> p g j", p=P), in_=result)
 
         deal_w8(0)
@@ -375,7 +407,7 @@ def tile_list_pasta_crack_page_kernel(tc, tab_words, tab_scales, offs, wa, w4_wo
         round_z_on_scalar(0, 0)
         weave_last_row(1)
         lift(1, 0)
-        round_z(1, 0)
+        round_z_on_vector(1, 0)
         lift(0, 1)
         round_z_on_scalar(0, 1)
         quantise_z(0, 0)

from contextlib import ExitStack

import concourse.mybir as mybir

K, H, T, S, T2, NX = 1536, 1024, 2048, 512, 1024, 512
FLOPS = 2 * (2 * K * H * S + H * H * NX + H * T2 * NX)

F32 = mybir.dt.float32
BF16 = mybir.dt.bfloat16
I32 = mybir.dt.int32
U32 = mybir.dt.uint32
U16 = mybir.dt.uint16
U8 = mybir.dt.uint8
FP8X4 = mybir.dt.float8_e4m3fn_x4
FP4X4 = mybir.dt.float4_e2m1fn_x4
ALU = mybir.AluOpType
ACT = mybir.ActivationFunctionType

P = 128
PACK = 4
PASS = P * PACK
K_PASSES = K // PASS
H_PASSES = H // PASS
CW = 256
CHUNKS = NX // CW
W4_BYTES = 2 * PASS
QUADRANT_ORDER = (0, 2, 1, 3)


def tile_list_pasta_crack_page_kernel(tc, tab_words, tab_scales, offs, wa, w4_words, w4_scales, dough, wgs,
                                                page0, offs2, offs3, w8_words, w8_scales, floor_v, gain, lim, out):
    nc = tc.nc
    with ExitStack() as ctx:
        keep = ctx.enter_context(tc.tile_pool(name="keep", bufs=1))
        ring = ctx.enter_context(tc.tile_pool(name="ring", bufs=3))
        half = ctx.enter_context(tc.tile_pool(name="half", bufs=3))
        work = ctx.enter_context(tc.tile_pool(name="work", bufs=2))
        psum = ctx.enter_context(tc.psum_pool(name="psum", bufs=8))

        def kept(shape, dtype, name):
            return keep.tile(shape, dtype, name=name, align_bytes=64)

        def staged(shape, dtype, tag, bufs=3):
            return ring.tile(shape, dtype, name=tag, tag=tag, bufs=bufs, align_bytes=64)

        def rounded(cols):
            return half.tile([P, cols], BF16, name="rounded", align_bytes=64)

        def bank(cols):
            return psum.tile([P, cols], F32, name="bank")

        idx = kept([P, S // 16], U16, "idx")
        idx2 = kept([P, S // 16], U16, "idx2")
        idx3 = kept([P, NX // 16], U16, "idx3")

        tab_sc = keep.tile([P, K_PASSES, T], U8, name="tab_sc", tag="scale_rows", align_bytes=64)
        w4_sc_raw = staged([P, K_PASSES, H], U8, "w4_scale_slot", 1)
        nc.gpsimd.memset(tab_sc[:, 0, :].bitcast(I32), 0)
        nc.vector.memset(tab_sc[:, 1:K_PASSES, :].rearrange("p a c -> p (a c)").bitcast(I32), 0)
        nc.gpsimd.memset(w4_sc_raw[:].rearrange("p a c -> p (a c)").bitcast(I32), 0)

        def load_scale_rows(dst, src):
            for q in QUADRANT_ORDER:
                nc.sync.dma_start(out=dst[32 * q : 32 * q + 4].bitcast(I32),
                                  in_=src[:, 4 * q : 4 * q + 4, :].rearrange("a r c -> r a c").bitcast(I32))

        wa_raw, tab, w4_raw, page = {}, {}, {}, {}

        def load_wa(b, a):
            wa_raw[b, a] = staged([P, PACK, PASS], F32, "wa_slot")
            rows = wa[PASS * a : PASS * (a + 1), PASS * b : PASS * (b + 1)]
            nc.sync.dma_start(out=wa_raw[b, a][:], in_=rows.rearrange("(p j) c -> p j c", j=PACK))

        def load_tab(a, tile):
            tab[a] = tile
            nc.sync.dma_start(out=tile[:], in_=tab_words[a].rearrange("p t i -> p (t i)").bitcast(I32))

        def load_w4(b, tile):
            w4_raw[b] = tile
            columns = w4_words[:, :, W4_BYTES * b : W4_BYTES * (b + 1)]
            nc.sync.dma_start(out=tile[:].bitcast(I32), in_=columns.rearrange("a p c -> p a c").bitcast(I32))

        def load_page(b, t, tile):
            page[b, t] = tile
            rows = page0[PASS * b : PASS * (b + 1), :].rearrange("(p t) c -> p t c", t=PACK)
            nc.sync.dma_start(out=tile[:], in_=rows[:, t, :])

        nc.sync.dma_start(idx[:], offs)
        load_w4(0, kept([P, K_PASSES, W4_BYTES], U8, "w4_raw0"))
        load_scale_rows(tab_sc, tab_scales)
        load_wa(0, 0)
        load_tab(0, staged([P, T], I32, "tab_slot"))
        load_scale_rows(w4_sc_raw, w4_scales)
        load_wa(0, 1)
        load_wa(0, 2)
        load_tab(1, staged([P, T], I32, "tab_slot"))
        load_tab(2, staged([P, T], I32, "last_tab_slot", 1))

        wa_bf, wa_q, wa_s = {}, {}, {}

        def round_wa(b, a, tile):
            wa_bf[b, a] = tile
            nc.scalar.copy(out=tile[:].rearrange("p (t m j) -> p m j t", t=PACK, j=PACK),
                           in_=wa_raw[b, a][:].rearrange("p j (m t) -> p m j t", t=PACK))

        def quantise(src, cols, name):
            codes = kept([P, cols], U32, name + "_q")
            scales = kept([P, cols], U8, name + "_s")
            nc.vector.quantize_mx(out=codes[:].bitcast(FP8X4), scales=scales[:], in_=src[:])
            return codes, scales

        def quantise_wa(b, a):
            wa_q[b, a], wa_s[b, a] = quantise(wa_bf[b, a], PASS, "wa%d%d" % (b, a))

        v_q, v_s = {}, {}

        def gather_words(a):
            v_q[a] = kept([P, S], U32, "v_q%d" % a)
            nc.vector.tensor_copy(v_q[a][:], tab[a][:].bitcast(U32).indirect(idx[:]))

        def gather_scales(a):
            v_s[a] = kept([P, S], U8, "v_s%d" % a)
            nc.vector.tensor_copy(v_s[a][:], tab_sc[:, a, :].indirect(idx[:]))

        w4_dealt = {}

        def deal_w4(b, tag):
            w4_dealt[b] = staged([P, K_PASSES, W4_BYTES + PASS], U8, tag, 1)
            nc.vector.tensor_copy(out=w4_dealt[b][:, :, 0:W4_BYTES].bitcast(U16).rearrange("p a (t m) -> p a t m", t=PACK),
                                  in_=w4_raw[b][:].bitcast(U16).rearrange("p a (m t) -> p a t m", t=PACK))

        def deal_w4_scales(b):
            nc.vector.tensor_copy(out=w4_dealt[b][:, :, W4_BYTES : W4_BYTES + PASS].rearrange("p a (t m) -> p a t m", t=PACK),
                                  in_=w4_sc_raw[:, :, PASS * b : PASS * (b + 1)].rearrange("p a (m t) -> p a t m", t=PACK))

        round_wa(0, 0, rounded(PACK * PASS))
        for a in range(K_PASSES):
            gather_scales(a)
        deal_w4(0, "first_w4_slot")
        w8_sc_raw = keep.tile([P, H], U8, name="w8_sc_raw", tag="scale_rows", align_bytes=64)
        nc.gpsimd.memset(w8_sc_raw[:].bitcast(I32), 0)
        gather_words(0)
        round_wa(0, 1, rounded(PACK * PASS))
        quantise_wa(0, 0)
        deal_w4_scales(0)
        round_wa(0, 2, rounded(PACK * PASS))
        quantise_wa(0, 1)
        quantise_wa(0, 2)
        gather_words(1)
        gather_words(2)

        load_w4(1, staged([P, K_PASSES, W4_BYTES], U8, "tab_slot"))
        dough_rows = dough.rearrange("(b p t) s -> b p t s", b=H_PASSES, t=PACK)
        rows = {0: kept([P, PACK, S], F32, "rows_a")}
        nc.sync.dma_start(out=rows[0][:, 0, :], in_=dough_rows[0, :, 0, :])
        wgs_rows = wgs.rearrange("(v t) s -> v t s", t=PACK)
        wg_first = keep.tile([P, S], F32, name="wg_first", tag="wg_first", align_bytes=64)
        for q in range(4):
            nc.sync.dma_start(out=wg_first[32 * q : 32 * (q + 1)], in_=wgs_rows[:, 0, :])
        nc.sync.dma_start(idx2[:], offs2)
        load_page(0, 0, kept([P, T2], F32, "page00"))
        nc.sync.dma_start(idx3[:], offs3)
        nc.sync.dma_start(out=rows[0][:, 1:PACK, :], in_=dough_rows[0, :, 1:PACK, :])
        wg_rest = keep.tile([P, PACK - 1, S], F32, name="wg_rest", tag="late", align_bytes=64)
        for q in range(4):
            nc.sync.dma_start(out=wg_rest[32 * q : 32 * (q + 1)], in_=wgs_rows[:, 1:PACK, :])
        load_page(0, 1, kept([P, T2], F32, "page01"))
        for a in range(K_PASSES):
            load_wa(1, a)
        load_page(0, 2, staged([P, T2], F32, "tab_slot"))
        load_page(0, 3, staged([P, T2], F32, "tab_slot"))
        floor_t = kept([P, H_PASSES, PACK], F32, "floor_t")
        gain_t = kept([P, H_PASSES, PACK], F32, "gain_t")
        nc.sync.dma_start(out=floor_t[:], in_=floor_v.rearrange("(b p t) -> p b t", b=H_PASSES, t=PACK))
        nc.sync.dma_start(out=gain_t[:], in_=gain.rearrange("(b p t) -> p b t", b=H_PASSES, t=PACK))

        lim_t = {}

        def load_lim(mh, tag):
            lim_t[mh] = staged([P, PACK, NX], F32, tag, 1)
            nc.sync.dma_start(out=lim_t[mh][:], in_=lim[PASS * mh : PASS * (mh + 1), :].rearrange("(g p) j -> p g j", p=P))

        tiles = [(b, t) for b in range(H_PASSES) for t in range(PACK)]
        last_tile = len(tiles) - 1
        last_of_first_half = PACK - 1
        top, crack = {}, {}

        def readings(i):
            b, t = tiles[i]
            slow = bank(S)
            fast = bank(S)
            for a in range(K_PASSES):
                first, last = a == 0, a == K_PASSES - 1
                nc.tensor.matmul_mx(out=slow[:], lhsT=w4_dealt[b][:, a, 2 * P * t : 2 * P * (t + 1)].bitcast(FP4X4),
                                    lhsT_scale=w4_dealt[b][:, a, W4_BYTES + P * t : W4_BYTES + P * (t + 1)],
                                    rhs=v_q[a][:].bitcast(FP8X4), rhs_scale=v_s[a][:], start=first, stop=last)
                nc.tensor.matmul_mx(out=fast[:], lhsT=wa_q[b, a][:, P * t : P * (t + 1)].bitcast(FP8X4),
                                    lhsT_scale=wa_s[b, a][:, P * t : P * (t + 1)],
                                    rhs=v_q[a][:].bitcast(FP8X4), rhs_scale=v_s[a][:], start=first, stop=last)
            slow_sb = work.tile([P, S], F32, name="slow_sb")
            nc.scalar.copy(out=slow_sb[:], in_=slow[:])
            top[i] = work.tile([P, S], F32, name="top", bufs=4)
            nc.vector.tensor_tensor(top[i][:], fast[:], slow_sb[:], ALU.max)
            nc.scalar.activation(top[i][:], top[i][:], ACT.Tanh)

        def times_dough(i):
            b, t = tiles[i]
            if i == last_of_first_half:
                crack[i] = staged([P, S], F32, "last_wa_slot", 1)
            else:
                crack[i] = work.tile([P, S], F32, name="crack")
            engine = nc.vector if i in (0, last_of_first_half) else nc.gpsimd
            engine.tensor_tensor(crack[i][:], top[i][:], rows[b][:, t, :], ALU.mult)

        def put(i):
            b, t = tiles[i]
            weights = wg_rest[:, t - 1, :] if t > 0 else wg_first[:]
            nc.vector.tensor_tensor(page[b, t][:].indirect(idx2[:]), crack[i][:], weights, ALU.mult)

        x = {}

        def fetch(i):
            b, t = tiles[i]
            nc.vector.tensor_copy(rows[b][:, t, :], page[b, t][:].indirect(idx3[:]))

        def fetch_last(c):
            b, t = tiles[last_tile]
            nc.vector.tensor_copy(x[b, c][:, t, :], page[b, t][:].indirect(idx3[:, c * CW // 16 : (c + 1) * CW // 16]))

        def woven(tile):
            return tile.rearrange("p (c i t) -> p c t i", i=4, t=PACK)

        def by_rows(row_tiles):
            return row_tiles.rearrange("p t (c i) -> p c t i", i=4)

        x_bf, x_q, x_s = {}, {}, {}

        def round_x(b, c):
            x_bf[b, c] = rounded(PACK * CW)
            nc.scalar.copy(out=woven(x_bf[b, c][:]), in_=by_rows(x[b, c]))

        def quantise_x(b, c):
            x_q[b, c], x_s[b, c] = quantise(x_bf[b, c], CW, "x%d%d" % (b, c))

        page_rows, page_bf, page_q, page_s = {}, {}, {}, {}

        def round_page_row(i):
            b, t = tiles[i]
            if t == 0:
                page_rows[b] = work.tile([P, PACK, T2], BF16, name="planes", bufs=1)
            nc.scalar.copy(out=page_rows[b][:, t, :], in_=page[b, t][:])

        def weave_page(b, mh, row_count, tile):
            page_bf[b, mh] = tile
            nc.scalar.copy(out=woven(tile[:])[:, :, 0:row_count, :],
                           in_=by_rows(page_rows[b][:, 0:row_count, PASS * mh : PASS * (mh + 1)]))

        def weave_last_row(mh):
            b, t = tiles[last_tile]
            nc.scalar.copy(out=page_bf[b, mh][:].rearrange("p (m t) -> p m t", t=PACK)[:, :, t],
                           in_=page[b, t][:, PASS * mh : PASS * (mh + 1)])

        def quantise_page(b, mh):
            page_q[b, mh], page_s[b, mh] = quantise(page_bf[b, mh], PASS, "page%d%d" % (b, mh))

        readings(0)
        readings(1)
        times_dough(0)
        deal_w4(1, "last_tab_slot")
        deal_w4_scales(1)
        readings(2)

        load_page(1, 0, staged([P, T2], F32, "w4_scale_slot", 1))
        rows[1] = staged([P, PACK, S], F32, "tab_slot")
        nc.sync.dma_start(out=rows[1][:], in_=dough_rows[1])
        load_page(1, 1, kept([P, T2], F32, "page11"))
        load_page(1, 2, staged([P, T2], F32, "wa_slot"))
        load_page(1, 3, staged([P, T2], F32, "wa_slot"))
        for b in range(H_PASSES):
            for c in range(CHUNKS):
                x[b, c] = rows[b][:, :, c * CW : (c + 1) * CW]
        w8_raw = staged([P, H_PASSES, H], I32, "wa_slot")
        nc.sync.dma_start(out=w8_raw[:], in_=w8_words.rearrange("a p c i -> p a (c i)").bitcast(I32))
        for q in range(4):
            nc.sync.dma_start(out=w8_sc_raw[32 * q : 32 * q + 4 * H_PASSES, :].bitcast(I32),
                              in_=w8_scales[:, 4 * q : 4 * q + 4, :].bitcast(I32))

        def finish_tile(i):
            fetch(i)
            round_page_row(i)

        put(0)
        readings(3)
        load_lim(0, "first_w4_slot")
        for a in range(K_PASSES - 1):
            round_wa(1, a, rounded(PACK * PASS))
        round_wa(1, K_PASSES - 1, staged([P, PACK * PASS], BF16, "last_wa_slot", 1))
        times_dough(1)
        finish_tile(0)

        put(1)
        times_dough(2)
        finish_tile(1)

        put(2)
        for a in range(K_PASSES):
            quantise_wa(1, a)
        times_dough(3)
        readings(4)
        readings(5)
        finish_tile(2)

        put(3)
        times_dough(4)
        readings(6)
        readings(7)
        load_lim(1, "last_tab_slot")
        finish_tile(3)
        for c in range(CHUNKS):
            round_x(0, c)

        put(4)
        times_dough(5)
        finish_tile(4)
        for c in range(CHUNKS):
            quantise_x(0, c)
        weave_page(0, 0, PACK, rounded(PACK * PASS))

        put(5)
        times_dough(6)
        finish_tile(5)
        quantise_page(0, 0)
        weave_page(0, 1, PACK, rounded(PACK * PASS))

        put(6)
        times_dough(7)
        finish_tile(6)
        w8_s = keep.tile([P, H], U8, name="w8_s", tag="wg_first", align_bytes=64)
        nc.vector.tensor_copy(out=w8_s[:].rearrange("p (b t m) -> p b t m", b=H_PASSES, t=PACK),
                              in_=w8_sc_raw[:].rearrange("p (b m t) -> p b t m", b=H_PASSES, t=PACK))
        quantise_page(0, 1)
        for mh in range(T2 // PASS):
            weave_page(1, mh, PACK - 1, kept([P, PACK * PASS], BF16, "page_bf%d" % mh))

        put(last_tile)
        for c in range(CHUNKS):
            fetch_last(c)
            round_x(1, c)

        w8_q = keep.tile([P, H_PASSES, H], U32, name="w8_q", tag="late", align_bytes=64)

        def deal_w8(b):
            cols = slice(PASS * b, PASS * (b + 1))
            nc.vector.tensor_copy(out=w8_q[:, :, cols].rearrange("p a (t m) -> p a m t", t=PACK),
                                  in_=w8_raw[:, :, cols].bitcast(U32).rearrange("p a (m t) -> p a m t", t=PACK))

        def lift(b, c):
            for t in range(PACK):
                y = bank(CW)
                col = PASS * b + P * t
                for a in range(H_PASSES):
                    nc.tensor.matmul_mx(out=y[:], lhsT=w8_q[:, a, col : col + P].bitcast(FP8X4),
                                        lhsT_scale=w8_s[4 * a : P, col : col + P],
                                        rhs=x_q[a, c][:].bitcast(FP8X4), rhs_scale=x_s[a, c][:],
                                        start=(a == 0), stop=(a == H_PASSES - 1))
                nc.vector.scalar_tensor_tensor(x[b, c][:, t, :], y[:], floor_t[:, b, t : t + 1], x[b, c][:, t, :],
                                               ALU.max, ALU.add)

        z_bf, z_q, z_s = {}, {}, {}

        def round_z_on_vector(b, c):
            z_bf[b, c] = rounded(PACK * CW)
            gains = gain_t[:, b, :].unsqueeze(1).unsqueeze(3).to_broadcast([P, CW // 4, PACK, 4])
            nc.vector.tensor_tensor(woven(z_bf[b, c][:]), by_rows(x[b, c]), gains, ALU.mult)

        def round_z_on_scalar(b, c):
            z_rows = work.tile([P, PACK, CW], BF16, name="z_rows")
            for t in range(PACK):
                nc.scalar.activation(z_rows[:, t, :], x[b, c][:, t, :], ACT.Copy, scale=gain_t[:, b, t : t + 1])
            z_bf[b, c] = rounded(PACK * CW)
            nc.scalar.copy(out=woven(z_bf[b, c][:]), in_=by_rows(z_rows[:]))

        def quantise_z(b, c):
            z_q[b, c], z_s[b, c] = quantise(z_bf[b, c], CW, "z%d%d" % (b, c))

        def score(c, mh, g0, count):
            cols = slice(c * CW, (c + 1) * CW)
            e = psum.tile([P, count, CW], F32, name="bank")
            for g in range(g0, g0 + count):
                for b in range(H_PASSES):
                    nc.tensor.matmul_mx(out=e[:, g - g0, :], lhsT=page_q[b, mh][:, P * g : P * (g + 1)].bitcast(FP8X4),
                                        lhsT_scale=page_s[b, mh][:, P * g : P * (g + 1)],
                                        rhs=z_q[b, c][:].bitcast(FP8X4), rhs_scale=z_s[b, c][:],
                                        start=(b == 0), stop=(b == H_PASSES - 1))
            result = lim_t[mh][:, g0 : g0 + count, cols]
            nc.vector.tensor_tensor(result, e[:], result, ALU.min)
            nc.scalar.activation(result, result, ACT.Abs)
            row = PASS * mh + P * g0
            nc.sync.dma_start(out=out[row : row + count * P, cols].rearrange("(g p) j -> p g j", p=P), in_=result)

        deal_w8(0)
        quantise_x(1, 0)
        weave_last_row(0)
        deal_w8(1)
        quantise_x(1, 1)
        lift(0, 0)
        round_z_on_scalar(0, 0)
        weave_last_row(1)
        lift(1, 0)
        round_z_on_vector(1, 0)
        lift(0, 1)
        round_z_on_scalar(0, 1)
        quantise_z(0, 0)
        quantise_z(1, 0)
        quantise_page(1, 0)
        lift(1, 1)
        round_z_on_scalar(1, 1)
        score(0, 0, 0, 2)
        quantise_page(1, 1)
        score(0, 0, 2, 2)
        quantise_z(0, 1)
        score(0, 1, 0, 2)
        quantise_z(1, 1)
        score(0, 1, 2, 2)
        score(1, 0, 0, 2)
        score(1, 0, 2, 2)
        score(1, 1, 0, 2)
        score(1, 1, 2, 1)
        score(1, 1, 3, 1)
